import numpy as np, ml_dtypes
CORES = [23,119,17,113]
N = 4
BF = ml_dtypes.bfloat16
def gentries(a):
    return np.ascontiguousarray(a.reshape(8, 16, -1).transpose(0, 2, 1)).reshape(8, -1)
def gtable(e):
    e = np.asarray(e); return np.ascontiguousarray(e.reshape(8, -1, 16).transpose(0, 2, 1)).reshape(128, -1).astype(np.int32)
def f(rng, *shape):
    return (rng.standard_normal(shape, dtype=np.float32) * np.exp2(rng.integers(-2, 3, shape[:-1] + (1,)))).astype(BF)
def wide(rng, *shape):
    v = f(rng, *shape).astype(np.float32); k = shape[:-2] + (1, shape[-1])
    return (v * np.exp2(rng.integers(-6, 7, k)) * (rng.random(k) > 0.0625)).astype(BF)
V, D, C, R = 4096, 2, 64, 2
def ranks(t):
    return t.reshape(8, D, N, V).transpose(2, 0, 1, 3)
def globe(a, bl):
    out = np.zeros((N, 8, D * V), np.int64)
    for r in range(N):
        own = np.broadcast_to(r * V + np.arange(V), (8, V))
        ghosts = (np.arange(N)[:, None, None] * V + bl[:, :, r]).transpose(1, 0, 2).reshape(8, N * C)
        out[r] = np.take_along_axis(np.concatenate([own, ghosts], 1), a[r].reshape(8, D * V).astype(np.int64), 1)
    return out.reshape(N, 8, D, V).transpose(1, 2, 0, 3).reshape(8, D, N * V)
def unpack(nb, bl):
    return np.stack([gentries(t) for t in nb]).reshape(N, 8, D, V), np.stack([gentries(t) for t in bl]).reshape(N, 8, N, C)
def pack(rng, a, bl, v):
    o = np.argsort(rng.random(a.shape), 2); a = np.take_along_axis(a, o, 2); v = np.take_along_axis(v, o, 2)
    return {"nb": np.stack([gtable(t.reshape(8, D * V)) for t in a]), "bl": np.stack([gtable(t.reshape(8, N * C)) for t in bl]),
            "w": np.ascontiguousarray(v).reshape(N, 8, D * V).astype(np.float32).astype(BF), "x": f(rng, N, 128, V)}
def graphs(rng, p):
    bl = np.argsort(rng.random((N, 8, N, V)), axis=-1)[..., :C]
    a = np.full((N, 8, D, V), -1, np.int64)
    for g in range(8):
        for d in range(D):
            for r in range(N):
                for q in range(r):
                    o = rng.permutation(C); u = bl[r, g, q]; t = bl[q, g, r][o]
                    k = (a[r, g, d, u] < 0) & (a[q, g, d, t] < 0) & (rng.random(C) < p)
                    a[r, g, d, u[k]] = V + q * C + o[k]; a[q, g, d, t[k]] = V + r * C + np.flatnonzero(k)
            for r in range(N):
                e = rng.permutation(np.flatnonzero(a[r, g, d] < 0)); h = len(e) // 2
                a[r, g, d, e[:h]] = e[h:2 * h]; a[r, g, d, e[h:2 * h]] = e[:h]
                if len(e) > 2 * h: a[r, g, d, e[-1]] = (e[-1] + 1) % V
        for r in range(N):
            alias = np.full(V, -1, np.int64); alias[bl[r, g, r]] = V + r * C + np.arange(C)
            b = a[r, g]; n = np.where(b < V, alias[np.minimum(b, V - 1)], -1)
            a[r, g] = np.where((n >= 0) & (rng.random((D, V)) < 0.5), n, b)
    return a, bl
def both(a, bl, z):
    return np.array(ranks(np.take_along_axis(z, np.minimum(globe(a, bl), np.arange(N * V)), 2)))
def setup_inputs(rng):
    a, bl = graphs(rng, 0.6)
    return pack(rng, a, bl, both(a, bl, np.exp2(4 * rng.random((8, D, N * V)))))
def setup_inputs_ties(rng):
    a, bl = graphs(rng, 0.6); z = rng.integers(1, 4, (8, D, N * V)).astype(np.float64); z[rng.integers(0, 8)] = 1
    z *= np.exp2(rng.integers(-20, 21, (8, 1, 1)))
    return pack(rng, a, bl, both(a, bl, z))
def setup_inputs_borders(rng):
    a, bl = graphs(rng, 1.0); v = both(a, bl, np.exp2(3 * rng.random((8, D, N * V))))
    far = ranks(globe(a, bl) // V != np.arange(N * V) // V)
    return pack(rng, a, bl, v * np.where(far, 8, 1))
def setup_inputs_hubs(rng):
    a, bl = graphs(rng, 0.6); v = both(a, bl, np.exp2(4 * rng.random((8, D, N * V))))
    for r in range(N):
        for g in range(8):
            e = rng.permutation(V); h = e[:16]; leaves = e[16:V // 2]; b = a[r, g]; c = v[r, g]
            b[:, leaves] = h[rng.integers(0, 16, (D, len(leaves)))]
            b[0, h] = h[np.arange(16) ^ 1]; c[0, h] = 256
    return pack(rng, a, bl, v)
def setup_inputs_any(rng):
    bl = rng.integers(0, V, (N, 8, N, C)); bl[..., C // 2:] = bl[..., :1]; bl[..., 1] = 0; bl[..., 2] = V - 1
    a = rng.integers(0, V + N * C, (N, 8, D, V)); j = np.arange(V)
    a = np.where(ranks(globe(a, bl) == np.arange(N * V)), (j + 1) % V, a)
    o = rng.permutation(8); a[:, o[0]] = (j + 1) % V; a[:, o[1]] = j ^ 1
    for r in range(N):
        for g in o[2:5]:
            q = r ^ 1
            a[r, g, :, bl[r, g, q, 0]] = V + q * C + rng.choice(np.r_[0, C // 2:C], D)
    return pack(rng, a, bl, np.exp2(4 * rng.random((N, 8, D, V))))
def setup_inputs_spread(rng):
    a, bl = graphs(rng, 0.6); z = np.exp2(rng.integers(-3, 4, (8, D, N * V)) + rng.random((8, D, N * V)))
    d = pack(rng, a, bl, both(a, bl, z)); d["x"] = wide(rng, N, 128, V); return d
def check_inputs(d):
    bad = []
    if d["bl"].min() < 0 or d["bl"].max() >= V: bad.append("bl")
    if d["nb"].min() < 0 or d["nb"].max() >= V + N * C: bad.append("nb")
    if not bad and (globe(*unpack(d["nb"], d["bl"])) == np.arange(N * V)).any(): bad.append("own neighbour")
    u = d["w"].astype(np.float32)
    if not (np.isfinite(u).all() and (u > 0).all()): bad.append("w")
    v = np.abs(d["x"].astype(np.float32))
    if not np.isfinite(v).all(): bad.append("x")
    if not 4.0 * D * float(u.max()) * float(v.max()) < 2.0 ** 127: bad.append("range")
    return bad
def reference(nb, bl, w, x):
    i = np.arange(N * V); A = globe(*unpack(nb, bl))
    u = w.astype(np.float64).reshape(N, 8, D, V).transpose(1, 2, 0, 3).reshape(8, D, N * V)
    mate = np.tile(i, (8, 1)); free = np.ones((8, N * V), bool)
    for t in range(R):
        k = np.where(np.take_along_axis(free[:, None], A, 2), u, 0.0)
        P = np.take_along_axis(A, np.argmax(k, 1)[:, None], 1)[:, 0]
        P = np.where(free & (np.max(k, 1) > 0), P, -1)
        hit = (P >= 0) & (np.take_along_axis(P, np.maximum(P, 0), 1) == i)
        mate = np.where(hit, P, mate); free = free & ~hit
    two = mate != i; first = np.minimum(mate, i); rep = first == i
    num = (np.add.accumulate(rep.reshape(8, N, V).astype(np.int64), 2) - 1 + V * np.arange(N)[:, None]).reshape(8, N * V)
    cm = np.take_along_axis(num, first, 1).reshape(8, N, V)
    xx = np.ascontiguousarray(x.astype(np.float64).reshape(N, 8, 16, V).transpose(1, 2, 0, 3)).reshape(8, 16, N * V)
    X = xx + np.where(two[:, None], np.take_along_axis(xx, mate[:, None], 2), 0.0)
    s = np.zeros((8, 16, N * V))
    for d in range(D):
        s += u[:, d, None] * np.take_along_axis(X, A[:, d, None], 2)
    s = s + np.where(two[:, None], np.take_along_axis(s, mate[:, None], 2), 0.0)
    y = np.zeros((8, 16, N * V))
    for g in range(8):
        y[g][:, num[g, rep[g]]] = s[g][:, rep[g]]
    y = np.ascontiguousarray(y.reshape(8, 16, N, V).transpose(2, 0, 1, 3)).reshape(N, 128, V)
    return {"y": y.astype(np.float32), "cm": np.stack([gtable(cm[:, r]) for r in range(N)]).astype(np.float32)}

@@ -1,0 +1,413 @@
+import numpy as np
+from concourse.bass import DstId, RemoteDMATransfer
+from concourse.mybir import AluOpType, ActivationFunctionType
+
+V, C, N = 4096, 64, 4
+GH = V + N * C
+ZC = GH
+CH = 512
+DUMP = 512
+DMA_CHUNKS = (0, 1, 2)
+NV = 8
+
+SCRATCH = {}
+
+
+def _declare(names, cols, dtype, rows=128):
+    for n in names.split():
+        SCRATCH[n] = ("sbuf", [rows, cols] if isinstance(cols, int) else [rows] + list(cols), dtype)
+
+
+_declare("bli blg ioh ioa bla blb", 16, "int32")
+_declare("blu blgu blh bl15", 16, "uint16")
+_declare("nbb", 32, "uint16")
+_declare("nbi", 512, "int32")
+_declare("nbu", 512, "uint16")
+_declare("z", (2, 16, 16), "bfloat16")
+_declare("wb wbs", 512, "bfloat16")
+_declare("u1 uo u2 mo pos cl", 256, "uint16")
+_declare("u1f uof u2f dif tmp tm2 mof num inc cms ivb idm fd zz mant s4 s5 s6 nbm0 nbm1 tb0 tb1", 256, "float32")
+_declare("pf p1b p2b m1 m2 nr1 nr rep z1 fr sg b0 bz eb ebf s1 s2 s3 sx blm wbm0 wbm1", 256, "bfloat16")
+_declare("im", 256, "int32")
+_declare("ohf", 16, "float32")
+_declare("ohb", 16, "bfloat16")
+_declare("igh iga", 8, "int32")
+_declare("ghb", 8, "bfloat16")
+_declare("icc", 2, "int32")
+_declare("gcol gco2", 2, "float32")
+_declare("r8", 128, "bfloat16", 8)
+_declare("osel", 2048, "bfloat16")
+_declare("oself", 2048, "float32")
+_declare("bo nt idn", 128, "bfloat16")
+_declare("we wp wm", GH, "bfloat16")
+_declare("wn fx", GH, "float32")
+_declare("gat", 2 * V, "bfloat16")
+_declare("gatn g1", V, "float32")
+_declare("xc wr0", V, "bfloat16")
+_declare("xw", GH + 16, "bfloat16")
+_declare("sw", GH + 16, "float32")
+_declare("w8", V, "bfloat16", 8)
+_declare("yb", DUMP + V, "float32")
+for _i in range(8):
+    SCRATCH["ps%d" % _i] = ("psum", [128, 512], "float32")
+
+EXCH = ["x0", "x1", "x2", "xx", "x3", "x4", "x6", "x5"]
+LOADS = ["lbl", "lnb", "lw", "lx", "lwr", "lw8", "lr8", "sty", "stc"] + ["ad%d" % k for k in DMA_CHUNKS]
+SEMAPHORES = ["v", "a", "t", "q", "sent"] + EXCH + LOADS
+
+
+def link_engines(topo, cores, src):
+    on = [d for d in cores if d != src and topo.chip(d) == topo.chip(src)]
+    off = [d for d in cores if d != src and topo.chip(d) != topo.chip(src)]
+    out, used = {}, []
+    for d in off + on:
+        left = [e for e in topo.engines(src, d) if e not in used]
+        if d in on and off:
+            far = topo.engines(src, off[0])
+            left = [e for e in left if e not in far] or left
+        out[d] = left[:4]
+        used += out[d]
+    return out
+
+
+def rank_program(g, core, T, topo):
+    r = T.rank_of(core)
+    if r is None:
+        return
+    A = AluOpType
+    COPY = ActivationFunctionType.Copy
+    IDENT = ActivationFunctionType.Identity
+    cores = list(T.cores)
+    Q = {"v": g.vector, "a": g.scalar, "t": g.tensor, "g": g, "y": g.sync}
+    SEM = {"v": "v", "a": "a", "t": "t", "g": "q"}
+    cnt = {s: 0 for s in SEMAPHORES}
+    seen = {}
+
+    def wait(qn, deps):
+        best = {}
+        for d in deps:
+            if d is not None:
+                best[d[0]] = max(best.get(d[0], 0), d[1])
+        for s, n in best.items():
+            if seen.get((qn, s), 0) < n:
+                Q[qn].wait_ge(T.sem[s], n)
+                seen[(qn, s)] = n
+
+    def op(qn, fn, *args, deps=(), **kw):
+        wait(qn, deps)
+        fn(*args, **kw).then_inc(T.sem[SEM[qn]], 1)
+        cnt[SEM[qn]] += 1
+        return (SEM[qn], cnt[SEM[qn]])
+
+    def dma(qn, sem, out, in_, deps=(), **kw):
+        wait(qn, deps)
+        Q[qn].dma_start(out, in_, **kw).then_inc(T.sem[sem], 16)
+        cnt[sem] += 16
+        return (sem, cnt[sem])
+
+    def tt(o, a, b, f, *deps):
+        return op("v", g.vector.tensor_tensor, o, a, b, f, deps=deps)
+
+    def ts(o, a, s1, f, *deps):
+        return op("v", g.vector.tensor_scalar, o, a, s1, None, f, deps=deps)
+
+    def cp(o, a, *deps):
+        return op("v", g.vector.tensor_copy, o, a, deps=deps)
+
+    def acp(o, a, *deps, **kw):
+        return op("a", g.scalar.activation, o, a, COPY, deps=deps, **kw)
+
+    def plus(o, a, b, *deps, **kw):
+        return op("a", g.scalar.activation, o, a, IDENT, bias=b, deps=deps, **kw)
+
+    mine = link_engines(topo, cores, core)
+
+    def exchange(sem, src, piece, dst, place, *deps):
+        wait("g", deps)
+        tr = []
+        for q in range(N):
+            if q == r:
+                continue
+            d = cores[q]
+            a = topo.addr(d)
+            a0, a1 = piece(q)
+            tr.append(RemoteDMATransfer(dst_ids=[DstId(rid=a[0], pnc=a[1])],
+                                        dma_engine_mask=sum(1 << e for e in mine[d]), remote_sem=T.sem[sem],
+                                        srcs=[src[:, a0:a1]], dsts=[dst[:, place[0]:place[1]]]))
+        g.remote_dma_fused(tr, local_sem=T.sem.sent)
+        cnt["sent"] += sum(len(mine[d]) for d in mine)
+        cnt[sem] += sum(len(link_engines(topo, cores, c)[core]) for c in cores if c != core)
+        return (sem, cnt[sem])
+
+    def slots(q):
+        return (C * q, C * q + C)
+
+    own = slots(r)
+    GO = (V + C * r, V + C * r + C)
+
+    k_bl = dma("y", "lbl", T.bli[:], T.bl[:])
+    k_nb = dma("y", "lnb", T.nbi[:], T.nb[:])
+    dma("a", "lw", T.z[:, 0], T.w[0::2, :])
+    k_w = dma("a", "lw", T.z[:, 1], T.w[1::2, :])
+
+    q_gh = op("g", g.iota, T.igh[:], [[-16, 8]], 0, 1)
+    q_oh = op("g", g.iota, T.ioh[:], [[-1, 16]], 16, 1)
+    q_im = op("g", g.iota, T.im[:], [[0, 32], [16, 8]], 128, 1)
+    a_x0 = exchange("x0", T.bli, lambda q: (4 * q, 4 * q + 4), T.blg, (4 * r, 4 * r + 4), k_bl)
+    q1 = op("g", g.iota, T.bo[:], [[0, 128]], 1, 0, allow_small_or_imprecise_dtypes=True)
+    q2 = op("g", g.affine_select, T.bo[:], T.bo[:], [[-16, 8], [0, 16]], A.is_ge, 0.0, 0, 1, deps=[q1])
+    q_bo = op("g", g.affine_select, T.bo[:], T.bo[:], [[16, 8], [0, 16]], A.is_ge, 0.0, 15, -1, deps=[q2])
+    q_vb = op("g", g.iota, T.ivb[:], [[16, 256]], 0, 1, allow_small_or_imprecise_dtypes=True)
+    q_dm = op("g", g.iota, T.idm[:], [[0, 8], [16, 32]], 0, 1, allow_small_or_imprecise_dtypes=True)
+    q_nt = op("g", g.affine_select, T.nt[:], T.bo[:], [[-1, 128]], A.is_ge, 0.0, 0, 1, deps=[q_bo])
+    q_id = op("g", g.affine_select, T.idn[:], T.bo[:], [[-1, 128]], A.is_equal, 0.0, 0, 1, deps=[q_bo])
+
+    v0 = op("v", g.vector.memset, T.zz[:], 0.0)
+    a0 = op("v", g.vector.memset, T.osel[:, 0:1024], 0.0)
+    c1 = ts(T.iga[:], T.igh[:], 4, A.arith_shift_right, q_gh)
+    c4 = ts(T.ghb[:], T.iga[:], 0, A.is_equal, c1)
+    v1 = op("v", g.vector.memset, T.fd[:], 1.0)
+    v2 = op("v", g.vector.memset, T.fd[:, 8:256:8], 2.0, deps=[v1])
+    c2 = ts(T.icc[:, 0:1], T.igh[:, 0:1], 15, A.bitwise_and, q_gh)
+    c3 = ts(T.ioa[:], T.ioh[:], 15, A.bitwise_and, q_oh)
+    fe = op("v", g.vector.tensor_tensor_scan, T.ps7[:, 0:256], T.fd[:], T.zz[:], float(2.0 ** (32 * r - 71)), A.mult, A.add, deps=[v2, v0])
+    c5 = tt(T.gcol[:, 0:1], T.icc[:, 0:1], T.igh[:, 0:1], A.subtract, c2)
+    c6 = ts(T.ohf[:], T.ioa[:], 0, A.is_equal, c3)
+    c7 = ts(T.ohb[:], T.ioa[:], 0, A.is_equal, c3)
+    mt = ts(T.mant[:], T.im[:], T.gcol[:, 0:1], A.add, q_im, c5)
+    eb = tt(T.eb[:], T.mant[:], T.ps7[:, 0:256], A.mult, mt, fe)
+
+    for c in range(4, 8):
+        a1 = acp(T.osel[:, 256 * c:256 * c + 256], T.zz[:], v0)
+    for c in range(16):
+        k_os = acp(T.osel[:, 129 * c:128 * (c + 1):16], T.ghb[:], c4, a0, a1)
+
+    def build(win, src, c_src, nv=NV, blocks=range(16)):
+        tv = ta = None
+        for c in blocks:
+            if c < nv:
+                tv = ts(win[:, c:V:16], src[:], T.ohb[:, c:c + 1], A.mult, c_src, c7)
+            else:
+                ta = acp(win[:, c:V:16], src[:], c_src, c6, scale=T.ohf[:, c:c + 1])
+        return [x for x in (tv, ta) if x is not None]
+
+    k_we = build(T.we, T.eb, eb, nv=6)
+
+    b1 = cp(T.blu[:], T.bli[:], k_bl)
+    b2 = cp(T.blg[:, 4 * r:4 * r + 4], T.bli[:, 4 * r:4 * r + 4])
+    for b in range(16):
+        k_wb = op("v", g.vector.transpose, T.wb[:, b:512:16], T.z[:, :, b, :], deps=[k_w])
+    d1 = tt(T.ps5[:, 0:256], T.nbi[:, 0:256], T.nbi[:, 256:512], A.subtract, k_nb)
+    d2 = tt(T.pf[:], T.wb[:, 0:256], T.wb[:, 256:512], A.is_ge, k_wb)
+    d3 = tt(T.ps5[:, 256:512], T.pf[:], T.ps5[:, 0:256], A.mult, d2, d1)
+    d4 = tt(T.u1f[:], T.nbi[:, 256:512], T.ps5[:, 256:512], A.add, d3)
+    k_u1 = cp(T.u1[:], T.u1f[:], d4)
+    b3 = cp(T.blgu[:], T.blg[:], a_x0, b2)
+    for q in range(N):
+        out, src = T.we[:, V + C * q:V + C * q + C], T.we[:, 0:V].indirect(T.blgu[:, 4 * q:4 * q + 4])
+        f = float(2.0 ** (32 * (q - r)))
+        if q < 2:
+            k_e1 = op("v", g.vector.tensor_scalar, out, src, f, None, A.mult, deps=[b3] + k_we)
+        else:
+            k_e2 = acp(out, src, b3, *k_we, scale=f)
+    k_we2 = k_we + [k_e1, k_e2]
+
+    k_sh = []
+
+    def shown(out, tile, *deps):
+        return tt(out[:], tile.indirect(T.blh[:]), T.blm[:], A.mult, *k_sh, *deps)
+
+    dma("y", "lx", T.xw[:, 0:V], T.x[:], [a_x0])
+    k_x = dma("y", "lx", T.xc[:], T.x[:])
+
+    PARTS = [("a", 144, 64), ("v", 0, 80), ("a", 208, 48), ("v", 80, 64)]
+
+    def lookup(win, lst, deps, ps, gat, g0, sel, parts=PARTS, psdeps=()):
+        tok = None
+        for e, k0, nk in parts:
+            out = gat[:, g0 + 16 * k0:g0 + 16 * (k0 + nk)]
+            src = win[:].indirect(lst[:, k0:k0 + nk])
+            x = cp(out, src, *deps) if e == "v" else acp(out, src, *deps)
+            wait("t", [x, k_os] + list(psdeps))
+            for c in range(16):
+                args = (ps[:, k0:k0 + nk], sel[:, 128 * c:128 * c + 128], gat[:, g0 + 16 * k0 + c:g0 + 16 * (k0 + nk):16], c == 0, c == 15)
+                if c < 15:
+                    g.tensor.matmul(*args)
+                else:
+                    tok = op("t", g.tensor.matmul, *args)
+        return tok
+
+    k_p1 = lookup(T.we, T.u1, k_we2 + [k_u1], T.ps0, T.gat, 0, T.osel)
+    k_of = acp(T.oself[:], T.osel[:])
+    e1 = tt(T.uof[:], T.nbi[:, 0:256], T.ps5[:, 256:512], A.subtract, d3)
+    b4 = ts(T.bla[:], T.bli[:], 4, A.arith_shift_right)
+    b5 = ts(T.blb[:], T.bli[:], 15, A.bitwise_and)
+    b6 = cp(T.blh[:], T.bla[:], b4)
+    b7 = cp(T.bl15[:], T.blb[:], b5)
+    k_sh += [b6, cp(T.blm[:], T.ohb[:].indirect(T.bl15[:]), b7, c7)]
+    p1 = cp(T.p1b[:], T.ps0[:, 0:256], k_p1)
+    o1 = shown(T.s1, T.p1b[:], p1)
+    a_x1 = exchange("x1", T.s1, slots, T.wp, GO, o1)
+    k_r8 = dma("y", "lr8", T.r8[:], T.bo[0:128:16, :], [q_bo])
+    k_w1 = build(T.wp, T.p1b, p1)
+    k_uo = cp(T.uo[:], T.uof[:], e1)
+    z_1 = acp(T.wp[:, GO[0]:GO[1]], T.s1[:, own[0]:own[1]], o1)
+    lookup(T.we, T.uo, k_we2 + [k_uo], T.ps1, T.gat, V, T.osel, parts=[("v", 0, 64), ("a", 128, 64)])
+    k_um = ts(T.ps5[:, 256:512], T.u1f[:], float(-ZC), A.add, e1)
+    k_lt1 = tt(T.ps5[:, 0:256], T.ps0[:, 0:256], T.eb[:], A.is_lt)
+
+    k_r1 = lookup(T.wp, T.u1, k_w1 + [a_x1, z_1], T.ps2, T.gat, 0, T.osel)
+    nbs = [shown(T["nbm%d" % d], T.nbi[:, 256 * d:256 * d + 256]) for d in range(2)]
+    m1 = tt(T.m1[:], T.ps2[:, 0:256], T.eb[:], A.is_equal, k_r1)
+    o2 = shown(T.s2, T.m1[:], m1)
+    a_x2 = exchange("x2", T.s2, slots, T.wm, GO, o2)
+    for c in range(16):
+        k_wr = dma("y", "lwr", T.wr0[c:128:16, :], T.w[:, 0:V], [a_x1])
+    k_w8 = dma("y", "lw8", T.w8[:], T.w[:, V:2 * V])
+    for d in range(2):
+        wait("t", [nbs[d], k_of])
+        for c in range(16):
+            args = (T.ps6[:, 16 * d:16 * d + 16], T.oself[:, 128 * c:128 * c + 128], T["nbm%d" % d][:, c:256:16], c == 0, c == 15)
+            if c < 15:
+                g.tensor.matmul(*args)
+            else:
+                k_nm = op("t", g.tensor.matmul, *args)
+    k_wm = build(T.wm, T.m1, m1)
+    z_2 = acp(T.wm[:, GO[0]:GO[1]], T.s2[:, own[0]:own[1]], o2)
+    f1 = tt(T.tm2[:], T.m1[:], T.ps5[:, 256:512], A.mult, k_um)
+    k_nr1 = tt(T.nr1[:], T.m1[:], T.ps5[:, 0:256], A.mult, k_lt1)
+    k_po = lookup(T.we, T.uo, k_we2 + [k_uo], T.ps1, T.gat, V, T.osel, parts=[("v", 64, 64), ("a", 192, 64)])
+
+    k_a1 = lookup(T.wm, T.u1, k_wm + [a_x2, z_2], T.ps3, T.gat, 0, T.osel)
+    k_fr = plus(T.fr[:], T.m1[:], 1.0, m1, scale=-1.0)
+    k_sg = plus(T.sg[:], T.m1[:], 1.0, scale=-2.0)
+    ox = acp(T.sx[:], T.xw[:, 0:V].indirect(T.blu[:]), k_x, b1)
+    a_xx = exchange("xx", T.sx, slots, T.xw, GO, ox)
+    z_x = acp(T.xw[:, GO[0]:GO[1]], T.sx[:, own[0]:own[1]], ox)
+    c8 = ts(T.gco2[:, 0:1], T.gcol[:, 0:1], float(4096 * r - DUMP), A.add)
+    k_vb = plus(T.ps7[:, 0:256], T.ivb[:], T.gcol[:, 0:1], q_vb, eb)
+    vx = op("v", g.vector.memset, T.xw[:, ZC:ZC + 16], 0.0)
+    vs = op("v", g.vector.memset, T.sw[:, ZC:ZC + 16], 0.0)
+    k_a0 = tt(T.ps5[:, 0:256], T.fr[:], T.ps0[:, 0:256], A.mult, k_fr, k_nr1)
+    k_ef = tt(T.ebf[:], T.eb[:], T.sg[:], A.mult, k_sg)
+    k_d = tt(T.ps2[:, 256:512], T.u1f[:], T.uof[:], A.subtract)
+    k_b0 = tt(T.b0[:], T.fr[:], T.ps1[:, 0:256], A.mult, k_po)
+    h1 = ts(T.z1[:], T.ps3[:, 0:256], 0.0, A.is_equal, k_a1)
+    h2 = tt(T.bz[:], T.b0[:], T.ps3[:, 0:256], A.mult, k_b0)
+    h3 = tt(T.ps5[:, 256:512], T.z1[:], T.ps5[:, 0:256], A.mult, h1, k_a0, f1)
+    p2 = tt(T.p2b[:], T.bz[:], T.ps5[:, 256:512], A.add, h2, h3)
+    o3 = shown(T.s3, T.p2b[:], p2)
+    a_x3 = exchange("x3", T.s3, slots, T.wp, GO, o3)
+    k_w2 = build(T.wp, T.p2b, p2)
+    z_3 = acp(T.wp[:, GO[0]:GO[1]], T.s3[:, own[0]:own[1]], o3)
+    q_y1 = op("g", g.iota, T.yb[:, DUMP:DUMP + V // 2], [[0, V // 2]], 0, 0, allow_small_or_imprecise_dtypes=True)
+    i1 = tt(T.ps2[:, 256:512], T.z1[:], T.ps2[:, 256:512], A.mult, k_d)
+    k_nbb = cp(T.nbb[:], T.ps6[:, 0:32], k_nm)
+    i2 = tt(T.u2f[:], T.uof[:], T.ps2[:, 256:512], A.add, i1)
+    k_lt2 = tt(T.ps6[:, 256:512], T.p2b[:], T.eb[:], A.is_lt, k_nbb)
+    k_u2 = cp(T.u2[:], T.u2f[:], i2)
+    k_A = plus(T.ps1[:, 256:512], T.tm2[:], float(ZC), f1, p2)
+    k_B = plus(T.ps1[:, 0:256], T.u2f[:], float(-ZC), i2)
+
+    k_r2 = lookup(T.wp, T.u2, k_w2 + [a_x3, z_3, k_u2], T.ps2, T.gat, 0, T.osel)
+    y0 = shown(T.wbm0, T.wb[:, 0:256])
+    y1 = shown(T.wbm1, T.wb[:, 256:512])
+    m2 = tt(T.m2[:], T.ps2[:, 0:256], T.ebf[:], A.is_equal, k_r2, k_ef)
+    j1 = tt(T.tmp[:], T.m2[:], T.ps1[:, 0:256], A.mult, m2, k_B)
+    j2 = tt(T.mof[:], T.tmp[:], T.ps1[:, 256:512], A.add, j1, k_A)
+    k_mo = cp(T.mo[:], T.mof[:], j2)
+
+    NC = V // CH
+    KC = CH // 16
+    CA = 448
+    FD = V - 3 * CA
+    dep_x = [k_mo, k_x, a_xx, z_x, vx]
+    k_fv = tt(T.fx[:, 0:FD], T.xw[:].indirect(T.mo[:, 0:FD // 16]), T.xc[:, 0:FD], A.add, *dep_x)
+    banks = [T.ps0, T.ps1, T.ps3]
+    sls = [slice(FD + CA * j, FD + CA * (j + 1)) for j in range(3)]
+    px = []
+    for j, sl in enumerate(sls):
+        gx = acp(T.gat[:, sl], T.xw[:].indirect(T.mo[:, sl.start // 16:sl.stop // 16]), *dep_x)
+        wait("t", [q_id, k_x, p2])
+        g.tensor.matmul(banks[j][:, 0:CA], T.idn[:], T.xc[:, sl], True, False)
+        px.append(op("t", g.tensor.matmul, banks[j][:, 0:CA], T.idn[:], T.gat[:, sl], False, True, deps=[gx]))
+        if j >= 1:
+            k_fa = acp(T.fx[:, sls[j - 1]], banks[j - 1][:, 0:CA], px[j - 1])
+    k_fa = acp(T.fx[:, sls[2]], banks[2][:, 0:CA], px[2])
+    r1 = tt(T.ps5[:, 0:256], T.m2[:], T.ps6[:, 256:512], A.mult, k_lt2, j2)
+    o4 = cp(T.s4[:], T.fx[:, 0:V].indirect(T.blu[:]), k_fv, k_fa)
+    a_x4 = exchange("x4", T.s4, slots, T.fx, GO, o4)
+    op("t", g.tensor.matmul, T.ps4[:, 0:256], T.bo[:], T.wbm0[:], True, True, deps=[y0, y1, q_bo])
+    k_pw = op("t", g.tensor.matmul, T.ps4[:, 256:512], T.bo[:], T.wbm1[:], True, True)
+    z_4 = acp(T.fx[:, GO[0]:GO[1]], T.s4[:, own[0]:own[1]], o4)
+    k_ws = acp(T.wbs[:], T.ps4[:], k_pw)
+
+    r2 = tt(T.nr[:], T.nr1[:], T.ps5[:, 0:256], A.add, r1, k_nr1)
+    l1 = tt(T.ps5[:, 256:512], T.mof[:], T.ps7[:, 0:256], A.subtract, k_vb)
+    k_rep = ts(T.rep[:], T.nr[:], 0.0, A.is_equal, r2)
+    op("t", g.tensor.matmul, T.ps6[:, 0:256], T.bo[:], T.rep[:], True, True, deps=[k_rep])
+    k_pn = op("t", g.tensor.matmul, T.ps6[:, 256:512], T.nt[:], T.rep[:], True, True, deps=[q_nt])
+    l2 = tt(T.dif[:], T.nr[:], T.ps5[:, 256:512], A.mult, l1)
+    k_nbu = cp(T.nbu[:], T.nbi[:])
+    k_in = op("v", g.vector.tensor_tensor_scan, T.inc[:], T.ps6[:, 0:256], T.zz[:], float(4096 * r), A.add, A.add, deps=[k_pn])
+    l3 = tt(T.tmp[:], T.dif[:], T.ps7[:, 0:256], A.add, l2)
+    k_num = tt(T.num[:], T.inc[:], T.ps6[:, 256:512], A.subtract, k_in)
+    k_cl = cp(T.cl[:], T.tmp[:], l3)
+    o6 = shown(T.s6, T.num[:], k_num)
+    a_x6 = exchange("x6", T.s6, slots, T.wn, GO, o6)
+    k_wn = build(T.wn, T.num, k_num, nv=0, blocks=range(8))
+
+    dep_f = [k_fv, k_fa, a_x4, z_4]
+    tb = [tt(T["tb%d" % d][:], T.fx[:].indirect(T.nbb[:, 16 * d:16 * d + 16]), T.wbs[:, 256 * d:256 * d + 256], A.mult, k_nbb, k_ws, *dep_f)
+          for d in range(2)]
+    t0, mm, ss, gg, pw, free = {}, {}, {}, {}, {}, {}
+    for i in range(NC + 2):
+        if i == NC:
+            k_wn = build(T.wn, T.num, k_num, nv=0, blocks=range(8, 16))
+            z_6 = acp(T.wn[:, GO[0]:GO[1]], T.s6[:, own[0]:own[1]], o6)
+        if i < NC:
+            sl = slice(CH * i, CH * i + CH)
+            gg[i] = acp(T.g1[:, sl], T.fx[:].indirect(T.nbu[:, 256 + KC * i:256 + KC * (i + 1)]), k_nbu, *dep_f)
+            pw[i] = op("t", g.tensor.matmul, T["ps%d" % (i % 2)][:], T.r8[:], T.w8[:, sl], True, True, deps=[k_r8, k_w8, k_fa, mm.get(i - 2)])
+            t0[i] = tt(T.sw[:, sl], T.fx[:].indirect(T.nbu[:, KC * i:KC * (i + 1)]), T.wr0[:, sl], A.mult, k_wr, *dep_f)
+        if i == 0:
+            o5 = tt(T.s5[:], T.tb0[:], T.tb1[:], A.add, *tb)
+            a_x5 = exchange("x5", T.s5, slots, T.sw, GO, o5)
+        k = i - 1
+        if 0 <= k < NC:
+            sl = slice(CH * k, CH * k + CH)
+            dst = T.g1[:, sl] if k in DMA_CHUNKS else T["ps%d" % (2 + k % 3)][:]
+            mm[k] = tt(dst, T.g1[:, sl], T["ps%d" % (k % 2)][:], A.mult, gg[k], pw[k], k_ws, free.get(k - 3))
+            if k in DMA_CHUNKS:
+                ss[k] = dma("g", "ad%d" % k, T.sw[:, sl], T.g1[:, sl], [t0[k], mm[k]], accum_op=A.add)
+        k = i - 2
+        if 0 <= k < NC and k not in DMA_CHUNKS:
+            sl = slice(CH * k, CH * k + CH)
+            ss[k] = free[k] = tt(T.sw[:, sl], T.sw[:, sl], T["ps%d" % (2 + k % 3)][:], A.add, t0[k], mm[k])
+    q_y2 = op("g", g.iota, T.yb[:, DUMP + V // 2:DUMP + V], [[0, V // 2]], 0, 0, allow_small_or_imprecise_dtypes=True)
+
+    k_dm = plus(T.ps6[:, 0:256], T.idm[:], T.gcol[:, 0:1], q_dm, k_num)
+    k_dmo = plus(T.ps6[:, 256:512], T.idm[:], T.gco2[:, 0:1], c8)
+    z_5 = acp(T.sw[:, GO[0]:GO[1]], T.s5[:, own[0]:own[1]], o5)
+
+    def coarse(parts):
+        return lookup(T.wn, T.cl, k_wn + [a_x6, z_6, k_cl], T.ps7, T.gatn, 0, T.oself, parts=[("a", 64 * j, 64) for j in parts], psdeps=[k_of, l3])
+
+    coarse((0, 1))
+    l4 = tt(T.ps5[:, 0:256], T.num[:], T.ps6[:, 256:512], A.subtract, k_dmo)
+    l5 = tt(T.mant[:], T.rep[:], T.ps5[:, 0:256], A.mult, l4)
+    l6 = tt(T.inc[:], T.mant[:], T.ps6[:, 0:256], A.add, l5, k_dm)
+    k_pos = cp(T.pos[:], T.inc[:], l6)
+
+    w = None
+    cuts = [CH * i for i in range(NC, 0, -1)] + [128, 0]
+    for n, (hi, lo) in enumerate(zip(cuts, cuts[1:])):
+        sl = slice(lo, hi)
+        x = acp(T.g1[:, sl], T.sw[:].indirect(T.mo[:, lo // 16:hi // 16]), a_x5, z_5, vs, mm[NC - 1], k_mo, *ss.values())
+        w = tt(T.yb[:, 0:DUMP + hi].indirect(T.pos[:, lo // 16:hi // 16]), T.sw[:, sl], T.g1[:, sl], A.add, x, w, k_pos, q_y1, q_y2, *ss.values())
+        k_y = dma("y", "sty", T.y[:, sl], T.yb[:, DUMP + lo:DUMP + hi], [w])
+        if n in (2, 4):
+            k_cm = coarse((2 + n // 4,))
+    k_c = acp(T.cms[:], T.ps7[:, 0:256], k_cm)
+    k_st = dma("y", "stc", T.cm[:], T.cms[:], [k_c])
+    wait("y", [(s, cnt[s]) for s in SEMAPHORES if cnt[s]])

@@ -3,12 +3,21 @@ from concourse.bass import DstId, RemoteDMATransfer
 from concourse.mybir import AluOpType, ActivationFunctionType
 
 V, C, N = 4096, 64, 4
-GH = V + N * C
+SL = N * C
+KS = SL // 16
+K = KS + V // 16
+GH = V + SL
 ZC = GH
 CH = 512
 DUMP = 512
 DMA_CHUNKS = (0, 1, 2)
-NV = 8
+N_V = 96
+A_CUT = (16, 80, 140, 206, K)
+B_CUT = (0, 64, 128, 200, K)
+B_END = 96
+C_CUT = (0, 64, 136, 208, K)
+X_CUT = (136, 160, 184, 208)
+COARSE = {-1: (0, 1), 2: (2,), 4: (3,)}
 
 SCRATCH = {}
 
@@ -19,40 +28,41 @@ def _declare(names, cols, dtype, rows=128):
 
 
 _declare("bli blg ioh ioa bla blb", 16, "int32")
-_declare("blu blgu blh bl15", 16, "uint16")
-_declare("nbb", 32, "uint16")
+_declare("blu blgu blh bl15 ob", 16, "uint16")
+_declare("obf", 16, "float32")
 _declare("nbi", 512, "int32")
 _declare("nbu", 512, "uint16")
 _declare("z", (2, 16, 16), "bfloat16")
-_declare("wb wbs", 512, "bfloat16")
-_declare("u1 uo u2 mo pos cl", 256, "uint16")
-_declare("u1f uof u2f dif tmp tm2 mof num inc cms ivb idm fd zz mant s4 s5 s6 nbm0 nbm1 tb0 tb1", 256, "float32")
-_declare("pf p1b p2b m1 m2 nr1 nr rep z1 fr sg b0 bz eb ebf s1 s2 s3 sx blm wbm0 wbm1", 256, "bfloat16")
-_declare("im", 256, "int32")
+_declare("wb wbs wx wbm", 512, "bfloat16")
+_declare("hl cl mo", K, "uint16")
+_declare("hf om dd cand cz mz nh", K, "float32")
+_declare("eb", K, "bfloat16")
+_declare("pos", 256, "uint16")
+_declare("num inc cms idm dm zz s5 s6 tb0 tb1 ge", 256, "float32")
+_declare("nbm", 512, "float32")
+_declare("pf sg rep blm", 256, "bfloat16")
 _declare("ohf", 16, "float32")
 _declare("ohb", 16, "bfloat16")
-_declare("igh iga", 8, "int32")
-_declare("ghb", 8, "bfloat16")
-_declare("icc", 2, "int32")
-_declare("gcol gco2", 2, "float32")
+_declare("igh icc", 2, "int32")
+_declare("gcol", 2, "float32")
 _declare("r8", 128, "bfloat16", 8)
-_declare("osel", 2048, "bfloat16")
-_declare("oself", 2048, "float32")
-_declare("bo nt idn", 128, "bfloat16")
-_declare("we wp wm", GH, "bfloat16")
-_declare("wn fx", GH, "float32")
-_declare("gat", 2 * V, "bfloat16")
+_declare("sel", 144, "bfloat16")
+_declare("one", 144, "float32")
+_declare("bo nt idn e0", 128, "bfloat16")
+_declare("we wa wh wc", SL + GH, "bfloat16")
+_declare("gat xc", SL + V, "bfloat16")
+_declare("gx wr0", V, "bfloat16")
+_declare("fx", SL + GH, "float32")
+_declare("wn sw", GH + 16, "float32")
 _declare("gatn g1", V, "float32")
-_declare("xc wr0", V, "bfloat16")
 _declare("xw", GH + 16, "bfloat16")
-_declare("sw", GH + 16, "float32")
 _declare("w8", V, "bfloat16", 8)
 _declare("yb", DUMP + V, "float32")
 for _i in range(8):
     SCRATCH["ps%d" % _i] = ("psum", [128, 512], "float32")
 
-EXCH = ["x0", "x1", "x2", "xx", "x3", "x4", "x6", "x5"]
-LOADS = ["lbl", "lnb", "lw", "lx", "lwr", "lw8", "lr8", "sty", "stc"] + ["ad%d" % k for k in DMA_CHUNKS]
+EXCH = ["x0", "x1", "x2", "x3", "xx", "x4", "x5", "x6"]
+LOADS = ["lbl", "lbo", "lnb", "lw", "lx", "lxc", "lwr", "lw8", "lr8", "sty", "stc"] + ["ad%d" % k for k in range(8)]
 SEMAPHORES = ["v", "a", "t", "q", "sent"] + EXCH + LOADS
 
 
@@ -82,332 +92,396 @@ def rank_program(g, core, T, topo):
     SEM = {"v": "v", "a": "a", "t": "t", "g": "q"}
     cnt = {s: 0 for s in SEMAPHORES}
     seen = {}
+    touched = {n: [] for n in SCRATCH}
+
+    def s(name, lo=0, hi=None, step=1, rows=None):
+        hi = SCRATCH[name][1][1] if hi is None else hi
+        return (T[name][slice(None) if rows is None else rows, lo:hi:step], [(name, lo, hi)])
+
+    def at(win, lst):
+        return (win[0].indirect(lst[0]), win[1], lst[1])
+
+    def hbm(ap):
+        return (ap, [])
 
     def wait(qn, deps):
         best = {}
-        for d in deps:
-            if d is not None:
-                best[d[0]] = max(best.get(d[0], 0), d[1])
-        for s, n in best.items():
-            if seen.get((qn, s), 0) < n:
-                Q[qn].wait_ge(T.sem[s], n)
-                seen[(qn, s)] = n
+        for sem, n in deps:
+            best[sem] = max(best.get(sem, 0), cnt[sem] if sem in LOADS else n)
+        for sem, n in best.items():
+            if seen.get((qn, sem), 0) < n:
+                Q[qn].wait_ge(T.sem[sem], n)
+                seen[(qn, sem)] = n
 
-    def op(qn, fn, *args, deps=(), **kw):
-        wait(qn, deps)
-        fn(*args, **kw).then_inc(T.sem[SEM[qn]], 1)
-        cnt[SEM[qn]] += 1
-        return (SEM[qn], cnt[SEM[qn]])
+    def spans(outs, ins):
+        views = [x for x in ins if isinstance(x, tuple)]
+        return [x for o in outs for x in o[1]], [x for i in views for x in i[1]] + [x for i in outs + views if len(i) > 2 for x in i[2]]
 
-    def dma(qn, sem, out, in_, deps=(), **kw):
-        wait(qn, deps)
-        Q[qn].dma_start(out, in_, **kw).then_inc(T.sem[sem], 16)
-        cnt[sem] += 16
-        return (sem, cnt[sem])
+    def hazards(qn, outs, ins):
+        wr, rd = spans(outs, ins)
+        deps = []
+        for group, writing in ((wr, True), (rd, False)):
+            for name, lo, hi in group:
+                bank = SCRATCH[name][0] == "psum"
+                deps += [tok for a, b, tok, q, w in touched[name]
+                         if (bank and q != qn) or (a < hi and lo < b and (w or writing))]
+        return deps
 
-    def tt(o, a, b, f, *deps):
-        return op("v", g.vector.tensor_tensor, o, a, b, f, deps=deps)
+    def record(qn, outs, ins, tok):
+        wr, rd = spans(outs, ins)
+        for name, lo, hi in rd:
+            touched[name].append((lo, hi, tok, qn, False))
+        for name, lo, hi in wr:
+            touched[name].append((lo, hi, tok, qn, True))
+        return tok
 
-    def ts(o, a, s1, f, *deps):
-        return op("v", g.vector.tensor_scalar, o, a, s1, None, f, deps=deps)
+    def ap(x):
+        return x[0] if isinstance(x, tuple) else x
 
-    def cp(o, a, *deps):
-        return op("v", g.vector.tensor_copy, o, a, deps=deps)
+    def side_by_side(qn, calls):
+        wait(qn, [d for fn, out, args, kw in calls for d in hazards(qn, [out], list(args) + list(kw.values()))])
+        for fn, out, args, kw in calls:
+            fn(ap(out), *[ap(x) for x in args], **{k: ap(x) for k, x in kw.items()}).then_inc(T.sem[SEM[qn]], 1)
+            cnt[SEM[qn]] += 1
+        for fn, out, args, kw in calls:
+            record(qn, [out], list(args) + list(kw.values()), (SEM[qn], cnt[SEM[qn]]))
 
-    def acp(o, a, *deps, **kw):
-        return op("a", g.scalar.activation, o, a, COPY, deps=deps, **kw)
+    def op(qn, fn, out, *args, **kw):
+        side_by_side(qn, [(fn, out, args, kw)])
 
-    def plus(o, a, b, *deps, **kw):
-        return op("a", g.scalar.activation, o, a, IDENT, bias=b, deps=deps, **kw)
+    def dmas(qn, sem, pairs, after=(), **kw):
+        wait(qn, [d for o, i in pairs for d in hazards(qn, [o], [i])] + list(after))
+        for o, i in pairs:
+            Q[qn].dma_start(ap(o), ap(i), **kw).then_inc(T.sem[sem], 16)
+            cnt[sem] += 16
+        for o, i in pairs:
+            record(sem, [o], [i], (sem, cnt[sem]))
+
+    def mm(out, terms):
+        ins = [x for t in terms for x in t]
+        wait("t", hazards("t", [out], ins))
+        for i, (l, x) in enumerate(terms):
+            call = g.tensor.matmul(ap(out), ap(l), ap(x), i == 0, i == len(terms) - 1)
+        call.then_inc(T.sem.t, 1)
+        cnt["t"] += 1
+        record("t", [out], ins, ("t", cnt["t"]))
+
+    def tt(o, a, b, f):
+        op("v", g.vector.tensor_tensor, o, a, b, f)
+
+    def ts(o, a, s1, f):
+        op("v", g.vector.tensor_scalar, o, a, s1, None, f)
+
+    def cp(o, a):
+        op("v", g.vector.tensor_copy, o, a)
+
+    def fill(o, c):
+        op("v", g.vector.memset, o, c)
+
+    def acp(o, a, **kw):
+        op("a", g.scalar.activation, o, a, COPY, **kw)
+
+    def plus(o, a, b, **kw):
+        op("a", g.scalar.activation, o, a, IDENT, bias=b, **kw)
+
+    def take(e, o, a):
+        cp(o, a) if e == "v" else acp(o, a)
+
+    def iota(o, pattern, base, step):
+        op("g", g.iota, o, pattern, base, step, allow_small_or_imprecise_dtypes=True)
+
+    def select(o, a, pattern, f, base, step):
+        op("g", g.affine_select, o, a, pattern, f, 0.0, base, step)
 
     mine = link_engines(topo, cores, core)
 
-    def exchange(sem, src, piece, dst, place, *deps):
-        wait("g", deps)
+    def exchange(sem, src, dst, d0, width=C):
+        pieces = [s(src, width * q, width * q + width) for q in range(N)]
+        wait("g", hazards("g", [], pieces))
         tr = []
         for q in range(N):
-            if q == r:
-                continue
-            d = cores[q]
-            a = topo.addr(d)
-            a0, a1 = piece(q)
-            tr.append(RemoteDMATransfer(dst_ids=[DstId(rid=a[0], pnc=a[1])],
-                                        dma_engine_mask=sum(1 << e for e in mine[d]), remote_sem=T.sem[sem],
-                                        srcs=[src[:, a0:a1]], dsts=[dst[:, place[0]:place[1]]]))
+            if q != r:
+                a = topo.addr(cores[q])
+                tr.append(RemoteDMATransfer(dst_ids=[DstId(rid=a[0], pnc=a[1])], remote_sem=T.sem[sem],
+                                            dma_engine_mask=sum(1 << e for e in mine[cores[q]]), srcs=[ap(pieces[q])],
+                                            dsts=[ap(s(dst, d0 + width * r, d0 + width * r + width))]))
         g.remote_dma_fused(tr, local_sem=T.sem.sent)
         cnt["sent"] += sum(len(mine[d]) for d in mine)
         cnt[sem] += sum(len(link_engines(topo, cores, c)[core]) for c in cores if c != core)
+        record(sem, [s(dst, d0 + width * q, d0 + width * q + width) for q in range(N) if q != r], [], (sem, cnt[sem]))
         return (sem, cnt[sem])
 
-    def slots(q):
-        return (C * q, C * q + C)
+    def keep(e, src, dst, d0):
+        take(e, s(dst, d0 + C * r, d0 + C * r + C), s(src, C * r, C * r + C))
 
-    own = slots(r)
-    GO = (V + C * r, V + C * r + C)
+    def win(name):
+        return s(name, SL, SL + GH)
 
-    k_bl = dma("y", "lbl", T.bli[:], T.bl[:])
-    k_nb = dma("y", "lnb", T.nbi[:], T.nb[:])
-    dma("a", "lw", T.z[:, 0], T.w[0::2, :])
-    k_w = dma("a", "lw", T.z[:, 1], T.w[1::2, :])
+    def row(name, k0, k1):
+        return s(name, 16 * k0, 16 * k1)
 
-    q_gh = op("g", g.iota, T.igh[:], [[-16, 8]], 0, 1)
-    q_oh = op("g", g.iota, T.ioh[:], [[-1, 16]], 16, 1)
-    q_im = op("g", g.iota, T.im[:], [[0, 32], [16, 8]], 128, 1)
-    a_x0 = exchange("x0", T.bli, lambda q: (4 * q, 4 * q + 4), T.blg, (4 * r, 4 * r + 4), k_bl)
-    q1 = op("g", g.iota, T.bo[:], [[0, 128]], 1, 0, allow_small_or_imprecise_dtypes=True)
-    q2 = op("g", g.affine_select, T.bo[:], T.bo[:], [[-16, 8], [0, 16]], A.is_ge, 0.0, 0, 1, deps=[q1])
-    q_bo = op("g", g.affine_select, T.bo[:], T.bo[:], [[16, 8], [0, 16]], A.is_ge, 0.0, 15, -1, deps=[q2])
-    q_vb = op("g", g.iota, T.ivb[:], [[16, 256]], 0, 1, allow_small_or_imprecise_dtypes=True)
-    q_dm = op("g", g.iota, T.idm[:], [[0, 8], [16, 32]], 0, 1, allow_small_or_imprecise_dtypes=True)
-    q_nt = op("g", g.affine_select, T.nt[:], T.bo[:], [[-1, 128]], A.is_ge, 0.0, 0, 1, deps=[q_bo])
-    q_id = op("g", g.affine_select, T.idn[:], T.bo[:], [[-1, 128]], A.is_equal, 0.0, 0, 1, deps=[q_bo])
+    def to_list(out, src, k0, k1, sel="sel"):
+        mm(out, [(s(sel, 15 - c, 143 - c), s(src, 16 * k0 + c, 16 * k1, 16)) for c in range(16)])
 
-    v0 = op("v", g.vector.memset, T.zz[:], 0.0)
-    a0 = op("v", g.vector.memset, T.osel[:, 0:1024], 0.0)
-    c1 = ts(T.iga[:], T.igh[:], 4, A.arith_shift_right, q_gh)
-    c4 = ts(T.ghb[:], T.iga[:], 0, A.is_equal, c1)
-    v1 = op("v", g.vector.memset, T.fd[:], 1.0)
-    v2 = op("v", g.vector.memset, T.fd[:, 8:256:8], 2.0, deps=[v1])
-    c2 = ts(T.icc[:, 0:1], T.igh[:, 0:1], 15, A.bitwise_and, q_gh)
-    c3 = ts(T.ioa[:], T.ioh[:], 15, A.bitwise_and, q_oh)
-    fe = op("v", g.vector.tensor_tensor_scan, T.ps7[:, 0:256], T.fd[:], T.zz[:], float(2.0 ** (32 * r - 71)), A.mult, A.add, deps=[v2, v0])
-    c5 = tt(T.gcol[:, 0:1], T.icc[:, 0:1], T.igh[:, 0:1], A.subtract, c2)
-    c6 = ts(T.ohf[:], T.ioa[:], 0, A.is_equal, c3)
-    c7 = ts(T.ohb[:], T.ioa[:], 0, A.is_equal, c3)
-    mt = ts(T.mant[:], T.im[:], T.gcol[:, 0:1], A.add, q_im, c5)
-    eb = tt(T.eb[:], T.mant[:], T.ps7[:, 0:256], A.mult, mt, fe)
+    def shown(out, tile):
+        tt(out, at(tile, s("blh")), s("blm"), A.mult)
 
-    for c in range(4, 8):
-        a1 = acp(T.osel[:, 256 * c:256 * c + 256], T.zz[:], v0)
-    for c in range(16):
-        k_os = acp(T.osel[:, 129 * c:128 * (c + 1):16], T.ghb[:], c4, a0, a1)
+    dmas("y", "lbl", [(s("bli"), hbm(T.bl[:]))])
+    dmas("a", "lw", [((T.z[:, h], [("z", h, h + 1)]), hbm(T.w[h::2, :])) for h in range(2)])
+    dmas("y", "lnb", [(s("nbi"), hbm(T.nb[:]))])
+    dmas("y", "lbo", [(s("blg", 4 * r, 4 * r + 4), hbm(T.bl[:, 4 * r:4 * r + 4]))])
 
-    def build(win, src, c_src, nv=NV, blocks=range(16)):
-        tv = ta = None
-        for c in blocks:
-            if c < nv:
-                tv = ts(win[:, c:V:16], src[:], T.ohb[:, c:c + 1], A.mult, c_src, c7)
-            else:
-                ta = acp(win[:, c:V:16], src[:], c_src, c6, scale=T.ohf[:, c:c + 1])
-        return [x for x in (tv, ta) if x is not None]
+    iota(s("e0"), [[1, 128]], 128, 0)
+    op("g", g.iota, s("igh"), [[0, 2]], 0, 1)
+    op("g", g.iota, s("ioh"), [[-1, 16]], 16, 1)
+    iota(s("one"), [[0, 144]], 0, 0)
+    iota(s("one", 15, 143, 16), [[0, 8]], 1, 0)
+    a_x0 = exchange("x0", "bli", "blg", 0, width=4)
+    select(s("one", 15, 143, 16), s("one", 15, 143, 16), [[-16, 8]], A.is_ge, 0, 1)
+    select(s("one", 15, 143, 16), s("one", 15, 143, 16), [[16, 8]], A.is_ge, 15, -1)
+    iota(s("bo"), [[0, 128]], 1, 0)
+    select(s("bo"), s("bo"), [[-16, 8], [0, 16]], A.is_ge, 0, 1)
+    select(s("bo"), s("bo"), [[16, 8], [0, 16]], A.is_ge, 15, -1)
+    iota(s("idm"), [[0, 8], [16, 32]], 0, 1)
+    select(s("nt"), s("bo"), [[-1, 128]], A.is_ge, 0, 1)
+    select(s("idn"), s("bo"), [[-1, 128]], A.is_equal, 0, 1)
 
-    k_we = build(T.we, T.eb, eb, nv=6)
+    E0 = 32 * r - 71
+    ts(s("we", SL, SL + 128), s("e0"), 2.0 ** E0, A.mult)
+    ts(s("we", SL + 128, SL + 256), s("e0"), 2.0 ** (E0 + 1), A.mult)
+    for n in (256, 512):
+        ts(s("we", SL + n, SL + 2 * n), s("we", SL, SL + n), 2.0 ** (n // 128), A.mult)
+    for n in (1024, 2048, 3072):
+        acp(s("we", SL + n, SL + n + 1024), s("we", SL, SL + 1024), scale=2.0 ** (n // 128))
+    ts(s("icc"), s("igh"), 15, A.bitwise_and)
+    ts(s("ioa"), s("ioh"), 15, A.bitwise_and)
+    cp(s("blu"), s("bli"))
+    ts(s("bla"), s("bli"), 4, A.arith_shift_right)
+    ts(s("blb"), s("bli"), 15, A.bitwise_and)
+    ts(s("ohb"), s("ioa"), 0, A.is_equal)
 
-    b1 = cp(T.blu[:], T.bli[:], k_bl)
-    b2 = cp(T.blg[:, 4 * r:4 * r + 4], T.bli[:, 4 * r:4 * r + 4])
-    for b in range(16):
-        k_wb = op("v", g.vector.transpose, T.wb[:, b:512:16], T.z[:, :, b, :], deps=[k_w])
-    d1 = tt(T.ps5[:, 0:256], T.nbi[:, 0:256], T.nbi[:, 256:512], A.subtract, k_nb)
-    d2 = tt(T.pf[:], T.wb[:, 0:256], T.wb[:, 256:512], A.is_ge, k_wb)
-    d3 = tt(T.ps5[:, 256:512], T.pf[:], T.ps5[:, 0:256], A.mult, d2, d1)
-    d4 = tt(T.u1f[:], T.nbi[:, 256:512], T.ps5[:, 256:512], A.add, d3)
-    k_u1 = cp(T.u1[:], T.u1f[:], d4)
-    b3 = cp(T.blgu[:], T.blg[:], a_x0, b2)
+    side_by_side("v", [(g.vector.transpose, s("wb", b, 512, 16), [(T.z[:, :, b, :], [("z", 0, 2)])], {}) for b in range(16)])
+    tt(s("ps5", 0, 256), s("nbi", 0, 256), s("nbi", 256, 512), A.subtract)
+    tt(s("pf"), s("wb", 0, 256), s("wb", 256, 512), A.is_ge)
+    cp(s("blh"), s("bla"))
+    tt(s("ps5", 256, 512), s("pf"), s("ps5", 0, 256), A.mult)
+    cp(s("bl15"), s("blb"))
+    tt(s("hf", KS), s("nbi", 256, 512), s("ps5", 256, 512), A.add)
+    cp(s("blgu"), s("blg"))
+    cp(s("hl", KS), s("hf", KS))
+    acp(s("sel"), s("one"), scale=0.0625)
+    to_list(s("ps7", KS, K), "we", KS, K)
+    plus(s("sg"), s("pf"), 1.0, scale=-2.0)
     for q in range(N):
-        out, src = T.we[:, V + C * q:V + C * q + C], T.we[:, 0:V].indirect(T.blgu[:, 4 * q:4 * q + 4])
-        f = float(2.0 ** (32 * (q - r)))
-        if q < 2:
-            k_e1 = op("v", g.vector.tensor_scalar, out, src, f, None, A.mult, deps=[b3] + k_we)
+        out, src = s("we", GH + C * q, GH + C * q + C), at(s("we", SL, GH), s("blgu", 4 * q, 4 * q + 4))
+        acp(out, src, scale=2.0 ** (32 * (q - r)))
+    dmas("y", "lx", [(s("xw", 0, V), hbm(T.x[:]))], [a_x0])
+    dmas("y", "lr8", [(s("r8"), s("bo", rows=slice(0, 128, 16)))])
+
+    acp(row("wa", KS + N_V, K), at(win("we"), s("hl", KS + N_V)))
+    cp(s("blm"), at(s("ohb"), s("bl15")))
+    tt(s("om", KS), s("sg"), s("ps5", 0, 256), A.mult)
+    shown(s("nbm", 0, 256), s("hf", KS))
+    shown(s("nbm", 256, 512), s("om", KS))
+    to_list(s("ps6", 0, 2 * KS), "nbm", 0, 2 * KS, "one")
+    cp(row("wa", KS, KS + N_V), at(win("we"), s("hl", KS, KS + N_V)))
+    cp(s("wa", 0, SL), at(s("wa", SL, GH), s("blu")))
+    a_x1 = exchange("x1", "wa", "wa", GH)
+    b0, b1, b2, b3, b4 = B_CUT
+    acp(s("we", 0, SL), at(s("we", SL, GH), s("blu")))
+    to_list(s("ps7", 0, KS), "we", 0, KS)
+    to_list(s("ps4", 0, K - b2), "wa", b2, K)
+    acp(s("xc", 0, SL), at(s("xw", 0, V), s("blu")))
+    exchange("xx", "xc", "xw", V)
+    keep("a", "wa", "wa", GH)
+    keep("a", "xc", "xw", V)
+    cp(s("hl", 0, KS), s("ps6", 0, KS))
+    cp(s("hf", 0, KS), s("ps6", 0, KS))
+    cp(s("om", 0, KS), s("ps6", KS, 2 * KS))
+    tt(s("wx", 0, 256), s("wb", 0, 256), s("wb", 256, 512), A.max)
+    tt(s("obf"), s("om", 0, KS), s("hf", 0, KS), A.add)
+    tt(s("wx", 256, 512), s("wb", 0, 256), s("wb", 256, 512), A.min)
+    cp(s("ob"), s("obf"))
+    shown(s("wbm", 0, 256), s("wx", 0, 256))
+    shown(s("wbm", 256, 512), s("wx", 256, 512))
+    acp(s("eb"), s("ps7", 0, K))
+    acp(s("nh", b2), s("ps4", 0, K - b2))
+    mm(s("ps5"), [(s("bo"), s("wbm"))])
+    acp(s("wbs"), s("ps5"))
+
+    cp(row("wh", 0, KS), at(win("wa"), s("hl", 0, KS)))
+    a_x2 = exchange("x2", "wh", "wh", GH)
+    dmas("y", "lxc", [(s("xc", SL), hbm(T.x[:]))], [a_x2])
+    a0, a1, a2, a3, a4 = A_CUT
+    for e, k0, k1, p0 in (("a", a2, a3, a2), ("v", a0, a1, 0), ("a", a3, a4, a3), ("v", a1, a2, a1)):
+        take(e, row("wh", k0, k1), at(win("wa"), s("hl", k0, k1)))
+        to_list(s("ps0", p0, k1), "wh", p0, k1)
+    keep("v", "wh", "wh", GH)
+
+    def ask(i):
+        k0, k1 = B_CUT[i:i + 2]
+        src = at(win("wh"), s("hl", k0, k1))
+        if k0 >= b2:
+            acp(row("gat", k0, k1), src)
         else:
-            k_e2 = acp(out, src, b3, *k_we, scale=f)
-    k_we2 = k_we + [k_e1, k_e2]
+            tt(row("gat", k0, k1), src, row("wa", k0, k1), A.is_equal)
+        to_list(s("ps%d" % (1 + i), 0, k1 - k0), "gat", k0, k1)
 
-    k_sh = []
+    def choose(i):
+        k0, k1 = B_CUT[i:i + 2]
+        ps, n, p0 = "ps%d" % (1 + i), k1 - k0, 0
+        if k0 >= b2:
+            p0 = 128
+            tt(s(ps, p0, p0 + n), s(ps, 0, n), s("nh", k0, k1), A.is_equal)
+        tt(s(ps, 256, 256 + n), s(ps, p0, p0 + n), s("dd", k0, k1), A.mult)
+        tt(s("cand", k0, k1), s(ps, 256, 256 + n), s("hf", k0, k1), A.add)
+        cp(s("cl", k0, k1), s("cand", k0, k1))
 
-    def shown(out, tile, *deps):
-        return tt(out[:], tile.indirect(T.blh[:]), T.blm[:], A.mult, *k_sh, *deps)
+    def name(e, k0, k1):
+        take(e, row("wc", k0, k1), at(win("we"), s("cl", k0, k1)))
 
-    dma("y", "lx", T.xw[:, 0:V], T.x[:], [a_x0])
-    k_x = dma("y", "lx", T.xc[:], T.x[:])
+    def order(k0, k1):
+        to_list(s("ps7", k0, k1), "wc", k0, k1)
 
-    PARTS = [("a", 144, 64), ("v", 0, 80), ("a", 208, 48), ("v", 80, 64)]
+    ask(0)
+    ask(2)
+    ask(3)
+    tt(s("ps5", 0, K), s("ps0", 0, K), s("eb"), A.not_equal)
+    tt(s("dd"), s("ps5", 0, K), s("om"), A.mult)
+    choose(0)
+    name("a", 0, KS)
+    a_x3 = exchange("x3", "wc", "wc", GH)
+    name("a", KS, b1)
+    ask(1)
+    choose(2)
+    name("a", b2, b3)
+    choose(3)
+    choose(1)
+    name("v", b1, b2)
+    name("a", b3, b3 + B_END // 2)
+    name("v", b3 + B_END // 2, b4)
+    keep("a", "wc", "wc", GH)
+    dmas("y", "lwr", [(s("wr0", rows=slice(c, 128, 16)), hbm(T.w[:, 0:V])) for c in range(16)], [a_x3])
+    dmas("y", "lw8", [(s("w8"), hbm(T.w[:, V:2 * V]))])
+    order(KS, b1)
+    order(b2, b3)
+    iota(s("yb", DUMP, DUMP + V // 2), [[0, V // 2]], 0, 0)
 
-    def lookup(win, lst, deps, ps, gat, g0, sel, parts=PARTS, psdeps=()):
-        tok = None
-        for e, k0, nk in parts:
-            out = gat[:, g0 + 16 * k0:g0 + 16 * (k0 + nk)]
-            src = win[:].indirect(lst[:, k0:k0 + nk])
-            x = cp(out, src, *deps) if e == "v" else acp(out, src, *deps)
-            wait("t", [x, k_os] + list(psdeps))
-            for c in range(16):
-                args = (ps[:, k0:k0 + nk], sel[:, 128 * c:128 * c + 128], gat[:, g0 + 16 * k0 + c:g0 + 16 * (k0 + nk):16], c == 0, c == 15)
-                if c < 15:
-                    g.tensor.matmul(*args)
-                else:
-                    tok = op("t", g.tensor.matmul, *args)
-        return tok
+    c0, c1, c2, c3, c4 = C_CUT
 
-    k_p1 = lookup(T.we, T.u1, k_we2 + [k_u1], T.ps0, T.gat, 0, T.osel)
-    k_of = acp(T.oself[:], T.osel[:])
-    e1 = tt(T.uof[:], T.nbi[:, 0:256], T.ps5[:, 256:512], A.subtract, d3)
-    b4 = ts(T.bla[:], T.bli[:], 4, A.arith_shift_right)
-    b5 = ts(T.blb[:], T.bli[:], 15, A.bitwise_and)
-    b6 = cp(T.blh[:], T.bla[:], b4)
-    b7 = cp(T.bl15[:], T.blb[:], b5)
-    k_sh += [b6, cp(T.blm[:], T.ohb[:].indirect(T.bl15[:]), b7, c7)]
-    p1 = cp(T.p1b[:], T.ps0[:, 0:256], k_p1)
-    o1 = shown(T.s1, T.p1b[:], p1)
-    a_x1 = exchange("x1", T.s1, slots, T.wp, GO, o1)
-    k_r8 = dma("y", "lr8", T.r8[:], T.bo[0:128:16, :], [q_bo])
-    k_w1 = build(T.wp, T.p1b, p1)
-    k_uo = cp(T.uo[:], T.uof[:], e1)
-    z_1 = acp(T.wp[:, GO[0]:GO[1]], T.s1[:, own[0]:own[1]], o1)
-    lookup(T.we, T.uo, k_we2 + [k_uo], T.ps1, T.gat, V, T.osel, parts=[("v", 0, 64), ("a", 128, 64)])
-    k_um = ts(T.ps5[:, 256:512], T.u1f[:], float(-ZC), A.add, e1)
-    k_lt1 = tt(T.ps5[:, 0:256], T.ps0[:, 0:256], T.eb[:], A.is_lt)
-
-    k_r1 = lookup(T.wp, T.u1, k_w1 + [a_x1, z_1], T.ps2, T.gat, 0, T.osel)
-    nbs = [shown(T["nbm%d" % d], T.nbi[:, 256 * d:256 * d + 256]) for d in range(2)]
-    m1 = tt(T.m1[:], T.ps2[:, 0:256], T.eb[:], A.is_equal, k_r1)
-    o2 = shown(T.s2, T.m1[:], m1)
-    a_x2 = exchange("x2", T.s2, slots, T.wm, GO, o2)
-    for c in range(16):
-        k_wr = dma("y", "lwr", T.wr0[c:128:16, :], T.w[:, 0:V], [a_x1])
-    k_w8 = dma("y", "lw8", T.w8[:], T.w[:, V:2 * V])
-    for d in range(2):
-        wait("t", [nbs[d], k_of])
-        for c in range(16):
-            args = (T.ps6[:, 16 * d:16 * d + 16], T.oself[:, 128 * c:128 * c + 128], T["nbm%d" % d][:, c:256:16], c == 0, c == 15)
-            if c < 15:
-                g.tensor.matmul(*args)
-            else:
-                k_nm = op("t", g.tensor.matmul, *args)
-    k_wm = build(T.wm, T.m1, m1)
-    z_2 = acp(T.wm[:, GO[0]:GO[1]], T.s2[:, own[0]:own[1]], o2)
-    f1 = tt(T.tm2[:], T.m1[:], T.ps5[:, 256:512], A.mult, k_um)
-    k_nr1 = tt(T.nr1[:], T.m1[:], T.ps5[:, 0:256], A.mult, k_lt1)
-    k_po = lookup(T.we, T.uo, k_we2 + [k_uo], T.ps1, T.gat, V, T.osel, parts=[("v", 64, 64), ("a", 192, 64)])
-
-    k_a1 = lookup(T.wm, T.u1, k_wm + [a_x2, z_2], T.ps3, T.gat, 0, T.osel)
-    k_fr = plus(T.fr[:], T.m1[:], 1.0, m1, scale=-1.0)
-    k_sg = plus(T.sg[:], T.m1[:], 1.0, scale=-2.0)
-    ox = acp(T.sx[:], T.xw[:, 0:V].indirect(T.blu[:]), k_x, b1)
-    a_xx = exchange("xx", T.sx, slots, T.xw, GO, ox)
-    z_x = acp(T.xw[:, GO[0]:GO[1]], T.sx[:, own[0]:own[1]], ox)
-    c8 = ts(T.gco2[:, 0:1], T.gcol[:, 0:1], float(4096 * r - DUMP), A.add)
-    k_vb = plus(T.ps7[:, 0:256], T.ivb[:], T.gcol[:, 0:1], q_vb, eb)
-    vx = op("v", g.vector.memset, T.xw[:, ZC:ZC + 16], 0.0)
-    vs = op("v", g.vector.memset, T.sw[:, ZC:ZC + 16], 0.0)
-    k_a0 = tt(T.ps5[:, 0:256], T.fr[:], T.ps0[:, 0:256], A.mult, k_fr, k_nr1)
-    k_ef = tt(T.ebf[:], T.eb[:], T.sg[:], A.mult, k_sg)
-    k_d = tt(T.ps2[:, 256:512], T.u1f[:], T.uof[:], A.subtract)
-    k_b0 = tt(T.b0[:], T.fr[:], T.ps1[:, 0:256], A.mult, k_po)
-    h1 = ts(T.z1[:], T.ps3[:, 0:256], 0.0, A.is_equal, k_a1)
-    h2 = tt(T.bz[:], T.b0[:], T.ps3[:, 0:256], A.mult, k_b0)
-    h3 = tt(T.ps5[:, 256:512], T.z1[:], T.ps5[:, 0:256], A.mult, h1, k_a0, f1)
-    p2 = tt(T.p2b[:], T.bz[:], T.ps5[:, 256:512], A.add, h2, h3)
-    o3 = shown(T.s3, T.p2b[:], p2)
-    a_x3 = exchange("x3", T.s3, slots, T.wp, GO, o3)
-    k_w2 = build(T.wp, T.p2b, p2)
-    z_3 = acp(T.wp[:, GO[0]:GO[1]], T.s3[:, own[0]:own[1]], o3)
-    q_y1 = op("g", g.iota, T.yb[:, DUMP:DUMP + V // 2], [[0, V // 2]], 0, 0, allow_small_or_imprecise_dtypes=True)
-    i1 = tt(T.ps2[:, 256:512], T.z1[:], T.ps2[:, 256:512], A.mult, k_d)
-    k_nbb = cp(T.nbb[:], T.ps6[:, 0:32], k_nm)
-    i2 = tt(T.u2f[:], T.uof[:], T.ps2[:, 256:512], A.add, i1)
-    k_lt2 = tt(T.ps6[:, 256:512], T.p2b[:], T.eb[:], A.is_lt, k_nbb)
-    k_u2 = cp(T.u2[:], T.u2f[:], i2)
-    k_A = plus(T.ps1[:, 256:512], T.tm2[:], float(ZC), f1, p2)
-    k_B = plus(T.ps1[:, 0:256], T.u2f[:], float(-ZC), i2)
-
-    k_r2 = lookup(T.wp, T.u2, k_w2 + [a_x3, z_3, k_u2], T.ps2, T.gat, 0, T.osel)
-    y0 = shown(T.wbm0, T.wb[:, 0:256])
-    y1 = shown(T.wbm1, T.wb[:, 256:512])
-    m2 = tt(T.m2[:], T.ps2[:, 0:256], T.ebf[:], A.is_equal, k_r2, k_ef)
-    j1 = tt(T.tmp[:], T.m2[:], T.ps1[:, 0:256], A.mult, m2, k_B)
-    j2 = tt(T.mof[:], T.tmp[:], T.ps1[:, 256:512], A.add, j1, k_A)
-    k_mo = cp(T.mo[:], T.mof[:], j2)
-
-    NC = V // CH
-    KC = CH // 16
-    CA = 448
-    FD = V - 3 * CA
-    dep_x = [k_mo, k_x, a_xx, z_x, vx]
-    k_fv = tt(T.fx[:, 0:FD], T.xw[:].indirect(T.mo[:, 0:FD // 16]), T.xc[:, 0:FD], A.add, *dep_x)
-    banks = [T.ps0, T.ps1, T.ps3]
-    sls = [slice(FD + CA * j, FD + CA * (j + 1)) for j in range(3)]
-    px = []
-    for j, sl in enumerate(sls):
-        gx = acp(T.gat[:, sl], T.xw[:].indirect(T.mo[:, sl.start // 16:sl.stop // 16]), *dep_x)
-        wait("t", [q_id, k_x, p2])
-        g.tensor.matmul(banks[j][:, 0:CA], T.idn[:], T.xc[:, sl], True, False)
-        px.append(op("t", g.tensor.matmul, banks[j][:, 0:CA], T.idn[:], T.gat[:, sl], False, True, deps=[gx]))
-        if j >= 1:
-            k_fa = acp(T.fx[:, sls[j - 1]], banks[j - 1][:, 0:CA], px[j - 1])
-    k_fa = acp(T.fx[:, sls[2]], banks[2][:, 0:CA], px[2])
-    r1 = tt(T.ps5[:, 0:256], T.m2[:], T.ps6[:, 256:512], A.mult, k_lt2, j2)
-    o4 = cp(T.s4[:], T.fx[:, 0:V].indirect(T.blu[:]), k_fv, k_fa)
-    a_x4 = exchange("x4", T.s4, slots, T.fx, GO, o4)
-    op("t", g.tensor.matmul, T.ps4[:, 0:256], T.bo[:], T.wbm0[:], True, True, deps=[y0, y1, q_bo])
-    k_pw = op("t", g.tensor.matmul, T.ps4[:, 256:512], T.bo[:], T.wbm1[:], True, True)
-    z_4 = acp(T.fx[:, GO[0]:GO[1]], T.s4[:, own[0]:own[1]], o4)
-    k_ws = acp(T.wbs[:], T.ps4[:], k_pw)
-
-    r2 = tt(T.nr[:], T.nr1[:], T.ps5[:, 0:256], A.add, r1, k_nr1)
-    l1 = tt(T.ps5[:, 256:512], T.mof[:], T.ps7[:, 0:256], A.subtract, k_vb)
-    k_rep = ts(T.rep[:], T.nr[:], 0.0, A.is_equal, r2)
-    op("t", g.tensor.matmul, T.ps6[:, 0:256], T.bo[:], T.rep[:], True, True, deps=[k_rep])
-    k_pn = op("t", g.tensor.matmul, T.ps6[:, 256:512], T.nt[:], T.rep[:], True, True, deps=[q_nt])
-    l2 = tt(T.dif[:], T.nr[:], T.ps5[:, 256:512], A.mult, l1)
-    k_nbu = cp(T.nbu[:], T.nbi[:])
-    k_in = op("v", g.vector.tensor_tensor_scan, T.inc[:], T.ps6[:, 0:256], T.zz[:], float(4096 * r), A.add, A.add, deps=[k_pn])
-    l3 = tt(T.tmp[:], T.dif[:], T.ps7[:, 0:256], A.add, l2)
-    k_num = tt(T.num[:], T.inc[:], T.ps6[:, 256:512], A.subtract, k_in)
-    k_cl = cp(T.cl[:], T.tmp[:], l3)
-    o6 = shown(T.s6, T.num[:], k_num)
-    a_x6 = exchange("x6", T.s6, slots, T.wn, GO, o6)
-    k_wn = build(T.wn, T.num, k_num, nv=0, blocks=range(8))
-
-    dep_f = [k_fv, k_fa, a_x4, z_4]
-    tb = [tt(T["tb%d" % d][:], T.fx[:].indirect(T.nbb[:, 16 * d:16 * d + 16]), T.wbs[:, 256 * d:256 * d + 256], A.mult, k_nbb, k_ws, *dep_f)
-          for d in range(2)]
-    t0, mm, ss, gg, pw, free = {}, {}, {}, {}, {}, {}
-    for i in range(NC + 2):
-        if i == NC:
-            k_wn = build(T.wn, T.num, k_num, nv=0, blocks=range(8, 16))
-            z_6 = acp(T.wn[:, GO[0]:GO[1]], T.s6[:, own[0]:own[1]], o6)
-        if i < NC:
-            sl = slice(CH * i, CH * i + CH)
-            gg[i] = acp(T.g1[:, sl], T.fx[:].indirect(T.nbu[:, 256 + KC * i:256 + KC * (i + 1)]), k_nbu, *dep_f)
-            pw[i] = op("t", g.tensor.matmul, T["ps%d" % (i % 2)][:], T.r8[:], T.w8[:, sl], True, True, deps=[k_r8, k_w8, k_fa, mm.get(i - 2)])
-            t0[i] = tt(T.sw[:, sl], T.fx[:].indirect(T.nbu[:, KC * i:KC * (i + 1)]), T.wr0[:, sl], A.mult, k_wr, *dep_f)
+    def answer(i):
+        k0, k1 = C_CUT[i:i + 2]
+        src = at(win("wc"), s("cl", k0, k1))
         if i == 0:
-            o5 = tt(T.s5[:], T.tb0[:], T.tb1[:], A.add, *tb)
-            a_x5 = exchange("x5", T.s5, slots, T.sw, GO, o5)
+            tt(row("gat", k0, k1), src, row("we", k0, k1), A.is_equal)
+        else:
+            acp(row("gat", k0, k1), src)
+        to_list(s("ps%d" % (1 + i), 0, k1 - k0), "gat", k0, k1)
+
+    def mates(i):
+        k0, k1 = C_CUT[i:i + 2]
+        ps, n, p0 = "ps%d" % (1 + i), k1 - k0, 0
+        if i > 0:
+            p0 = 128
+            tt(s(ps, p0, p0 + n), s(ps, 0, n), s("eb", k0, k1), A.is_equal)
+        tt(s("mz", k0, k1), s(ps, p0, p0 + n), s("cz", k0, k1), A.mult)
+        ts(s("mo", k0, k1), s("mz", k0, k1), float(ZC), A.add)
+
+    def joined(k0, k1):
+        tt(row("fx", k0, k1), at(s("xw"), s("mo", k0, k1)), row("xc", k0, k1), A.add)
+
+    answer(0)
+    answer(1)
+    ts(s("cz"), s("cand"), -float(ZC), A.add)
+    fill(s("xw", ZC), 0.0)
+    fill(s("sw", ZC), 0.0)
+    fill(s("wn", ZC), 65536.0)
+    fill(s("zz"), 0.0)
+    mates(0)
+    joined(0, KS)
+    exchange("x4", "fx", "fx", GH)
+    answer(2)
+    answer(3)
+    order(b1, b2)
+    order(b3, b4)
+    joined(KS, c1)
+    mates(1)
+    joined(c1, X_CUT[0])
+    mates(2)
+    banks = ["ps0", "ps1", "ps2"]
+    parts = list(zip(X_CUT, X_CUT[1:]))
+    for j, (k0, k1) in enumerate(parts):
+        n = 16 * (k1 - k0)
+        acp(s("gx", CH * j, CH * j + n), at(s("xw"), s("mo", k0, k1)))
+        mm(s(banks[j], 0, n), [(s("idn"), row("xc", k0, k1)), (s("idn"), s("gx", CH * j, CH * j + n))])
+        if j:
+            acp(row("fx", *parts[j - 1]), s(banks[j - 1], 0, 16 * (parts[j - 1][1] - parts[j - 1][0])))
+    mates(3)
+    if X_CUT[-1] < c3:
+        joined(X_CUT[-1], c3)
+    joined(c3, c4)
+    acp(row("fx", *parts[-1]), s(banks[-1], 0, 16 * (parts[-1][1] - parts[-1][0])))
+    keep("a", "fx", "fx", GH)
+
+    op("v", g.vector.tensor_tensor, s("ge"), s("ps7", KS, K), s("eb", KS), A.is_ge)
+    cp(s("nbu"), s("nbi"))
+    ts(s("ps5", 0, 256), s("ge"), -65536.0, A.mult)
+    tt(s("gcol"), s("icc"), s("igh"), A.subtract)
+    tt(s("rep"), s("mz", KS), s("ps5", 0, 256), A.is_ge)
+    ts(s("ohf"), s("ioa"), 0, A.is_equal)
+    mm(s("ps6", 0, 256), [(s("bo"), s("rep"))])
+    mm(s("ps6", 256, 512), [(s("nt"), s("rep"))])
+    tt(s("tb0"), at(win("fx"), s("hl", 0, KS)), s("wbs", 0, 256), A.mult)
+    op("v", g.vector.tensor_tensor_scan, s("inc"), s("ps6", 0, 256), s("zz"), float(V * r), A.add, A.add)
+    tt(s("tb1"), at(win("fx"), s("ob")), s("wbs", 256, 512), A.mult)
+    tt(s("num"), s("inc"), s("ps6", 256, 512), A.subtract)
+    tt(s("s5"), s("tb0"), s("tb1"), A.add)
+    exchange("x5", "s5", "sw", V)
+    shown(s("s6"), s("num"))
+    exchange("x6", "s6", "wn", V)
+
+    NC, KC = V // CH, CH // 16
+    for i in range(NC + 2):
+        if i < NC:
+            lo, hi = CH * i, CH * i + CH
+            acp(s("g1", lo, hi), at(win("fx"), s("nbu", 256 + KC * i, 256 + KC * (i + 1))))
+            mm(s("ps%d" % (i % 2)), [(s("r8"), s("w8", lo, hi))])
+            tt(s("sw", lo, hi), at(win("fx"), s("nbu", KC * i, KC * (i + 1))), s("wr0", lo, hi), A.mult)
         k = i - 1
         if 0 <= k < NC:
-            sl = slice(CH * k, CH * k + CH)
-            dst = T.g1[:, sl] if k in DMA_CHUNKS else T["ps%d" % (2 + k % 3)][:]
-            mm[k] = tt(dst, T.g1[:, sl], T["ps%d" % (k % 2)][:], A.mult, gg[k], pw[k], k_ws, free.get(k - 3))
+            lo, hi = CH * k, CH * k + CH
+            dst = s("g1", lo, hi) if k in DMA_CHUNKS else s("ps%d" % (2 + k % 3))
+            tt(dst, s("g1", lo, hi), s("ps%d" % (k % 2)), A.mult)
             if k in DMA_CHUNKS:
-                ss[k] = dma("g", "ad%d" % k, T.sw[:, sl], T.g1[:, sl], [t0[k], mm[k]], accum_op=A.add)
+                dmas("g", "ad%d" % k, [(s("sw", lo, hi), s("g1", lo, hi))], accum_op=A.add)
         k = i - 2
         if 0 <= k < NC and k not in DMA_CHUNKS:
-            sl = slice(CH * k, CH * k + CH)
-            ss[k] = free[k] = tt(T.sw[:, sl], T.sw[:, sl], T["ps%d" % (2 + k % 3)][:], A.add, t0[k], mm[k])
-    q_y2 = op("g", g.iota, T.yb[:, DUMP + V // 2:DUMP + V], [[0, V // 2]], 0, 0, allow_small_or_imprecise_dtypes=True)
+            lo, hi = CH * k, CH * k + CH
+            tt(s("sw", lo, hi), s("sw", lo, hi), s("ps%d" % (2 + k % 3)), A.add)
+    iota(s("yb", DUMP + V // 2), [[0, V // 2]], 0, 0)
+    keep("a", "s5", "sw", V)
+    keep("a", "s6", "wn", V)
+    plus(s("dm"), s("idm"), s("gcol", 0, 1))
+    plus(s("ps6", 0, 256), s("num"), float(DUMP - V * r))
+    side_by_side("a", [(g.scalar.activation, s("wn", c, V, 16), [s("num"), COPY], {"scale": s("ohf", c, c + 1)}) for c in range(16)])
 
-    k_dm = plus(T.ps6[:, 0:256], T.idm[:], T.gcol[:, 0:1], q_dm, k_num)
-    k_dmo = plus(T.ps6[:, 256:512], T.idm[:], T.gco2[:, 0:1], c8)
-    z_5 = acp(T.sw[:, GO[0]:GO[1]], T.s5[:, own[0]:own[1]], o5)
+    def coarse(n):
+        for j in COARSE.get(n, ()):
+            acp(s("gatn", 1024 * j, 1024 * j + 1024), at(s("wn"), s("mo", KS + 64 * j, KS + 64 * j + 64)))
+            to_list(s("ps7", 64 * j, 64 * j + 64), "gatn", 64 * j, 64 * j + 64, "one")
 
-    def coarse(parts):
-        return lookup(T.wn, T.cl, k_wn + [a_x6, z_6, k_cl], T.ps7, T.gatn, 0, T.oself, parts=[("a", 64 * j, 64) for j in parts], psdeps=[k_of, l3])
+    coarse(-1)
+    tt(s("inc"), s("rep"), s("ps6", 0, 256), A.mult)
+    tt(s("ps5", 0, 256), s("inc"), s("dm"), A.max)
+    cp(s("pos"), s("ps5", 0, 256))
 
-    coarse((0, 1))
-    l4 = tt(T.ps5[:, 0:256], T.num[:], T.ps6[:, 256:512], A.subtract, k_dmo)
-    l5 = tt(T.mant[:], T.rep[:], T.ps5[:, 0:256], A.mult, l4)
-    l6 = tt(T.inc[:], T.mant[:], T.ps6[:, 0:256], A.add, l5, k_dm)
-    k_pos = cp(T.pos[:], T.inc[:], l6)
-
-    w = None
     cuts = [CH * i for i in range(NC, 0, -1)] + [128, 0]
     for n, (hi, lo) in enumerate(zip(cuts, cuts[1:])):
-        sl = slice(lo, hi)
-        x = acp(T.g1[:, sl], T.sw[:].indirect(T.mo[:, lo // 16:hi // 16]), a_x5, z_5, vs, mm[NC - 1], k_mo, *ss.values())
-        w = tt(T.yb[:, 0:DUMP + hi].indirect(T.pos[:, lo // 16:hi // 16]), T.sw[:, sl], T.g1[:, sl], A.add, x, w, k_pos, q_y1, q_y2, *ss.values())
-        k_y = dma("y", "sty", T.y[:, sl], T.yb[:, DUMP + lo:DUMP + hi], [w])
-        if n in (2, 4):
-            k_cm = coarse((2 + n // 4,))
-    k_c = acp(T.cms[:], T.ps7[:, 0:256], k_cm)
-    k_st = dma("y", "stc", T.cm[:], T.cms[:], [k_c])
-    wait("y", [(s, cnt[s]) for s in SEMAPHORES if cnt[s]])
+        acp(s("g1", lo, hi), at(s("sw"), s("mo", KS + lo // 16, KS + hi // 16)))
+        tt(at(s("yb", 0, DUMP + hi), s("pos", lo // 16, hi // 16)), s("sw", lo, hi), s("g1", lo, hi), A.add)
+        dmas("y", "sty", [(hbm(T.y[:, lo:hi]), s("yb", DUMP + lo, DUMP + hi))])
+        coarse(n)
+        if n == 7:
+            tt(s("cms"), s("ps7", 0, 256), s("num"), A.min)
+            dmas("y", "stc", [(hbm(T.cm[:]), s("cms"))])
+    wait("y", [(n, cnt[n]) for n in SEMAPHORES if cnt[n]])

@@ -11,12 +11,12 @@ ZC = GH
 CH = 512
 DUMP = 512
 DMA_CHUNKS = (0, 1, 2)
-N_V = 96
+N_V = 128
 A_CUT = (16, 80, 140, 206, K)
 B_CUT = (0, 64, 128, 200, K)
-B_END = 96
+B_END = 248
 C_CUT = (0, 64, 136, 208, K)
-X_CUT = (136, 160, 184, 208)
+X_CUT = (64, 92, 120, 148)
 COARSE = {-1: (0, 1), 2: (2,), 4: (3,)}
 
 SCRATCH = {}
@@ -27,34 +27,37 @@ def _declare(names, cols, dtype, rows=128):
         SCRATCH[n] = ("sbuf", [rows, cols] if isinstance(cols, int) else [rows] + list(cols), dtype)
 
 
-_declare("bli blg ioh ioa bla blb", 16, "int32")
-_declare("blu blgu blh bl15 ob", 16, "uint16")
-_declare("obf", 16, "float32")
-_declare("nbi", 512, "int32")
-_declare("nbu", 512, "uint16")
+_declare("bli ioh ioa bla blb", 16, "int32")
+_declare("blu blh bl15", 16, "uint16")
+_declare("blg tl", 32, "uint16")
+_declare("ti", 32, "int32")
+_declare("z2", (16, 32), "bfloat16")
+_declare("nbi", 2 * K, "int32")
+_declare("nbu", 2 * K, "uint16")
 _declare("z", (2, 16, 16), "bfloat16")
-_declare("wb wbs wx wbm", 512, "bfloat16")
+_declare("wb wbm wt", 512, "bfloat16")
 _declare("hl cl mo", K, "uint16")
 _declare("hf om dd cand cz mz nh", K, "float32")
-_declare("eb", K, "bfloat16")
+_declare("eb pf sg", K, "bfloat16")
 _declare("pos", 256, "uint16")
-_declare("num inc cms idm dm zz s5 s6 tb0 tb1 ge", 256, "float32")
+_declare("num inc cms idm dm zz s5 s6 ge", 256, "float32")
 _declare("nbm", 512, "float32")
-_declare("pf sg rep blm", 256, "bfloat16")
+_declare("rep blm pfm", 256, "bfloat16")
 _declare("ohf", 16, "float32")
 _declare("ohb", 16, "bfloat16")
 _declare("igh icc", 2, "int32")
 _declare("gcol", 2, "float32")
 _declare("r8", 128, "bfloat16", 8)
-_declare("sel", 144, "bfloat16")
+_declare("sel oneb", 144, "bfloat16")
 _declare("one", 144, "float32")
 _declare("bo nt idn e0", 128, "bfloat16")
 _declare("we wa wh wc", SL + GH, "bfloat16")
-_declare("gat xc", SL + V, "bfloat16")
-_declare("gx wr0", V, "bfloat16")
+_declare("gat xc wr0", SL + V, "bfloat16")
+_declare("gx", V, "bfloat16")
 _declare("fx", SL + GH, "float32")
 _declare("wn sw", GH + 16, "float32")
-_declare("gatn g1", V, "float32")
+_declare("gatn", V, "float32")
+_declare("g1", SL + V, "float32")
 _declare("xw", GH + 16, "bfloat16")
 _declare("w8", V, "bfloat16", 8)
 _declare("yb", DUMP + V, "float32")
@@ -62,7 +65,7 @@ for _i in range(8):
     SCRATCH["ps%d" % _i] = ("psum", [128, 512], "float32")
 
 EXCH = ["x0", "x1", "x2", "x3", "xx", "x4", "x5", "x6"]
-LOADS = ["lbl", "lbo", "lnb", "lw", "lx", "lxc", "lwr", "lw8", "lr8", "sty", "stc"] + ["ad%d" % k for k in range(8)]
+LOADS = ["lbl", "lnb", "lw", "lx", "lxc", "lwr", "lw8", "lr8", "sty", "stc"] + ["ad%d" % k for k in range(8)]
 SEMAPHORES = ["v", "a", "t", "q", "sent"] + EXCH + LOADS
 
 
@@ -195,7 +198,7 @@ def rank_program(g, core, T, topo):
 
     mine = link_engines(topo, cores, core)
 
-    def exchange(sem, src, dst, d0, width=C):
+    def exchange(sem, src, dst, d0, width=C, pitch=C):
         pieces = [s(src, width * q, width * q + width) for q in range(N)]
         wait("g", hazards("g", [], pieces))
         tr = []
@@ -204,11 +207,11 @@ def rank_program(g, core, T, topo):
                 a = topo.addr(cores[q])
                 tr.append(RemoteDMATransfer(dst_ids=[DstId(rid=a[0], pnc=a[1])], remote_sem=T.sem[sem],
                                             dma_engine_mask=sum(1 << e for e in mine[cores[q]]), srcs=[ap(pieces[q])],
-                                            dsts=[ap(s(dst, d0 + width * r, d0 + width * r + width))]))
+                                            dsts=[ap(s(dst, d0 + pitch * r, d0 + pitch * r + width))]))
         g.remote_dma_fused(tr, local_sem=T.sem.sent)
         cnt["sent"] += sum(len(mine[d]) for d in mine)
         cnt[sem] += sum(len(link_engines(topo, cores, c)[core]) for c in cores if c != core)
-        record(sem, [s(dst, d0 + width * q, d0 + width * q + width) for q in range(N) if q != r], [], (sem, cnt[sem]))
+        record(sem, [s(dst, d0 + pitch * q, d0 + pitch * q + width) for q in range(N) if q != r], [], (sem, cnt[sem]))
         return (sem, cnt[sem])
 
     def keep(e, src, dst, d0):
@@ -227,18 +230,28 @@ def rank_program(g, core, T, topo):
         tt(out, at(tile, s("blh")), s("blm"), A.mult)
 
     dmas("y", "lbl", [(s("bli"), hbm(T.bl[:]))])
+    dmas("y", "lnb", [(s("nbi", K * d + KS, K * d + K), hbm(T.nb[:, 256 * d:256 * d + 256])) for d in range(2)])
     dmas("a", "lw", [((T.z[:, h], [("z", h, h + 1)]), hbm(T.w[h::2, :])) for h in range(2)])
-    dmas("y", "lnb", [(s("nbi"), hbm(T.nb[:]))])
-    dmas("y", "lbo", [(s("blg", 4 * r, 4 * r + 4), hbm(T.bl[:, 4 * r:4 * r + 4]))])
 
     iota(s("e0"), [[1, 128]], 128, 0)
-    op("g", g.iota, s("igh"), [[0, 2]], 0, 1)
     op("g", g.iota, s("ioh"), [[-1, 16]], 16, 1)
-    iota(s("one"), [[0, 144]], 0, 0)
-    iota(s("one", 15, 143, 16), [[0, 8]], 1, 0)
-    a_x0 = exchange("x0", "bli", "blg", 0, width=4)
+    op("g", g.iota, s("ti"), [[1, 32]], 0, 32)
+    fill(s("one"), 0.0)
+    fill(s("one", 15, 143, 16), 1.0)
     select(s("one", 15, 143, 16), s("one", 15, 143, 16), [[-16, 8]], A.is_ge, 0, 1)
     select(s("one", 15, 143, 16), s("one", 15, 143, 16), [[16, 8]], A.is_ge, 15, -1)
+    E0 = 32 * r - 71
+    ts(s("we", SL, SL + 128), s("e0"), 2.0 ** E0, A.mult)
+    ts(s("we", SL + 128, SL + 256), s("e0"), 2.0 ** (E0 + 1), A.mult)
+    ts(s("we", SL + 256, SL + 512), s("we", SL, SL + 256), 4.0, A.mult)
+    ts(s("ioa"), s("ioh"), 15, A.bitwise_and)
+    ts(s("we", SL + 512, SL + 1024), s("we", SL, SL + 512), 16.0, A.mult)
+    ts(s("ti"), s("ti"), 511, A.bitwise_and)
+    ts(s("ohb"), s("ioa"), 0, A.is_equal)
+    cp(s("tl"), s("ti"))
+    cp(s("blu"), s("bli"))
+    a_x0 = exchange("x0", "blu", "blg", 0, width=4, pitch=8)
+    op("g", g.iota, s("igh"), [[0, 2]], 0, 1)
     iota(s("bo"), [[0, 128]], 1, 0)
     select(s("bo"), s("bo"), [[-16, 8], [0, 16]], A.is_ge, 0, 1)
     select(s("bo"), s("bo"), [[16, 8], [0, 16]], A.is_ge, 15, -1)
@@ -246,68 +259,59 @@ def rank_program(g, core, T, topo):
     select(s("nt"), s("bo"), [[-1, 128]], A.is_ge, 0, 1)
     select(s("idn"), s("bo"), [[-1, 128]], A.is_equal, 0, 1)
 
-    E0 = 32 * r - 71
-    ts(s("we", SL, SL + 128), s("e0"), 2.0 ** E0, A.mult)
-    ts(s("we", SL + 128, SL + 256), s("e0"), 2.0 ** (E0 + 1), A.mult)
-    for n in (256, 512):
-        ts(s("we", SL + n, SL + 2 * n), s("we", SL, SL + n), 2.0 ** (n // 128), A.mult)
-    for n in (1024, 2048, 3072):
+    def names(n):
         acp(s("we", SL + n, SL + n + 1024), s("we", SL, SL + 1024), scale=2.0 ** (n // 128))
-    ts(s("icc"), s("igh"), 15, A.bitwise_and)
-    ts(s("ioa"), s("ioh"), 15, A.bitwise_and)
-    cp(s("blu"), s("bli"))
-    ts(s("bla"), s("bli"), 4, A.arith_shift_right)
-    ts(s("blb"), s("bli"), 15, A.bitwise_and)
-    ts(s("ohb"), s("ioa"), 0, A.is_equal)
 
-    side_by_side("v", [(g.vector.transpose, s("wb", b, 512, 16), [(T.z[:, :, b, :], [("z", 0, 2)])], {}) for b in range(16)])
-    tt(s("ps5", 0, 256), s("nbi", 0, 256), s("nbi", 256, 512), A.subtract)
-    tt(s("pf"), s("wb", 0, 256), s("wb", 256, 512), A.is_ge)
-    cp(s("blh"), s("bla"))
-    tt(s("ps5", 256, 512), s("pf"), s("ps5", 0, 256), A.mult)
+    names(1024)
+    side_by_side("a", [(g.scalar.activation, (T.z2[:, :, 16 * h:16 * h + 16], [("z2", 0, 1)]), [(T.z[:, h], [("z", h, h + 1)]), COPY], {})
+                       for h in range(2)])
+    acp(s("oneb"), s("one"))
+    ts(s("blb"), s("bli"), 15, A.bitwise_and)
+    ts(s("bla"), s("bli"), 4, A.arith_shift_right)
     cp(s("bl15"), s("blb"))
-    tt(s("hf", KS), s("nbi", 256, 512), s("ps5", 256, 512), A.add)
-    cp(s("blgu"), s("blg"))
-    cp(s("hl", KS), s("hf", KS))
+    cp(s("blh"), s("bla"))
+    cp(s("blm"), at(s("ohb"), s("bl15")))
+    op("v", g.vector.transpose, s("wt"), (T.z2[:], [("z2", 0, 1)]))
+    acp(s("wb", 256), at(s("wt"), s("tl", 16)))
+    cp(s("wb", 0, 256), at(s("wt"), s("tl", 0, 16)))
+    names(2048)
+    names(3072)
+    acp(s("we", 0, SL), at(s("we", SL, GH), s("blu")))
     acp(s("sel"), s("one"), scale=0.0625)
-    to_list(s("ps7", KS, K), "we", KS, K)
-    plus(s("sg"), s("pf"), 1.0, scale=-2.0)
+    keep("a", "we", "we", GH)
+    for d in range(2):
+        shown(s("nbm", 256 * d, 256 * d + 256), s("nbi", K * d + KS, K * d + K))
+    to_list(s("ps6", 0, 2 * KS), "nbm", 0, 2 * KS, "one")
+    tt(s("pf", KS), s("wb", 0, 256), s("wb", 256, 512), A.is_ge)
+    tt(s("ps5", KS, K), s("nbi", KS, K), s("nbi", K + KS), A.subtract)
+    shown(s("pfm"), s("pf", KS))
+    to_list(s("ps3", 0, KS), "pfm", 0, KS, "oneb")
+    to_list(s("ps7", 0, K), "we", 0, K)
+    tt(s("ps4", KS, K), s("pf", KS), s("ps5", KS, K), A.mult)
+    tt(s("hf", KS), s("nbi", K + KS), s("ps4", KS, K), A.add)
+    cp(s("hl", KS), s("hf", KS))
+    for d in range(2):
+        cp(s("nbi", K * d, K * d + KS), s("ps6", KS * d, KS * d + KS))
+    cp(s("pf", 0, KS), s("ps3", 0, KS))
+    tt(s("ps5", 0, KS), s("nbi", 0, KS), s("nbi", K, K + KS), A.subtract)
+    tt(s("ps4", 0, KS), s("pf", 0, KS), s("ps5", 0, KS), A.mult)
+    tt(s("hf", 0, KS), s("nbi", K, K + KS), s("ps4", 0, KS), A.add)
+    cp(s("hl", 0, KS), s("hf", 0, KS))
     for q in range(N):
-        out, src = s("we", GH + C * q, GH + C * q + C), at(s("we", SL, GH), s("blgu", 4 * q, 4 * q + 4))
-        acp(out, src, scale=2.0 ** (32 * (q - r)))
+        if q != r:
+            acp(s("we", GH + C * q, GH + C * q + C), at(s("we", SL, GH), s("blg", 8 * q, 8 * q + 4)), scale=2.0 ** (32 * (q - r)))
     dmas("y", "lx", [(s("xw", 0, V), hbm(T.x[:]))], [a_x0])
     dmas("y", "lr8", [(s("r8"), s("bo", rows=slice(0, 128, 16)))])
 
-    acp(row("wa", KS + N_V, K), at(win("we"), s("hl", KS + N_V)))
-    cp(s("blm"), at(s("ohb"), s("bl15")))
-    tt(s("om", KS), s("sg"), s("ps5", 0, 256), A.mult)
-    shown(s("nbm", 0, 256), s("hf", KS))
-    shown(s("nbm", 256, 512), s("om", KS))
-    to_list(s("ps6", 0, 2 * KS), "nbm", 0, 2 * KS, "one")
-    cp(row("wa", KS, KS + N_V), at(win("we"), s("hl", KS, KS + N_V)))
-    cp(s("wa", 0, SL), at(s("wa", SL, GH), s("blu")))
-    a_x1 = exchange("x1", "wa", "wa", GH)
     b0, b1, b2, b3, b4 = B_CUT
-    acp(s("we", 0, SL), at(s("we", SL, GH), s("blu")))
-    to_list(s("ps7", 0, KS), "we", 0, KS)
-    to_list(s("ps4", 0, K - b2), "wa", b2, K)
-    acp(s("xc", 0, SL), at(s("xw", 0, V), s("blu")))
-    exchange("xx", "xc", "xw", V)
-    keep("a", "wa", "wa", GH)
-    keep("a", "xc", "xw", V)
-    cp(s("hl", 0, KS), s("ps6", 0, KS))
-    cp(s("hf", 0, KS), s("ps6", 0, KS))
-    cp(s("om", 0, KS), s("ps6", KS, 2 * KS))
-    tt(s("wx", 0, 256), s("wb", 0, 256), s("wb", 256, 512), A.max)
-    tt(s("obf"), s("om", 0, KS), s("hf", 0, KS), A.add)
-    tt(s("wx", 256, 512), s("wb", 0, 256), s("wb", 256, 512), A.min)
-    cp(s("ob"), s("obf"))
-    shown(s("wbm", 0, 256), s("wx", 0, 256))
-    shown(s("wbm", 256, 512), s("wx", 256, 512))
+    acp(row("wa", N_V, K), at(win("we"), s("hl", N_V)))
+    cp(row("wa", 0, KS), at(win("we"), s("hl", 0, KS)))
+    a_x1 = exchange("x1", "wa", "wa", GH)
+    cp(row("wa", KS, N_V), at(win("we"), s("hl", KS, N_V)))
+    to_list(s("ps2", 0, K - b2), "wa", b2, K)
+    keep("v", "wa", "wa", GH)
+    plus(s("sg"), s("pf"), 1.0, scale=-2.0)
     acp(s("eb"), s("ps7", 0, K))
-    acp(s("nh", b2), s("ps4", 0, K - b2))
-    mm(s("ps5"), [(s("bo"), s("wbm"))])
-    acp(s("wbs"), s("ps5"))
 
     cp(row("wh", 0, KS), at(win("wa"), s("hl", 0, KS)))
     a_x2 = exchange("x2", "wh", "wh", GH)
@@ -316,7 +320,10 @@ def rank_program(g, core, T, topo):
     for e, k0, k1, p0 in (("a", a2, a3, a2), ("v", a0, a1, 0), ("a", a3, a4, a3), ("v", a1, a2, a1)):
         take(e, row("wh", k0, k1), at(win("wa"), s("hl", k0, k1)))
         to_list(s("ps0", p0, k1), "wh", p0, k1)
+        if k0 == a0:
+            tt(s("om"), s("sg"), s("ps5", 0, K), A.mult)
     keep("v", "wh", "wh", GH)
+    acp(s("nh", b2), s("ps2", 0, K - b2))
 
     def ask(i):
         k0, k1 = B_CUT[i:i + 2]
@@ -327,15 +334,17 @@ def rank_program(g, core, T, topo):
             tt(row("gat", k0, k1), src, row("wa", k0, k1), A.is_equal)
         to_list(s("ps%d" % (1 + i), 0, k1 - k0), "gat", k0, k1)
 
-    def choose(i):
-        k0, k1 = B_CUT[i:i + 2]
-        ps, n, p0 = "ps%d" % (1 + i), k1 - k0, 0
-        if k0 >= b2:
-            p0 = 128
-            tt(s(ps, p0, p0 + n), s(ps, 0, n), s("nh", k0, k1), A.is_equal)
-        tt(s(ps, 256, 256 + n), s(ps, p0, p0 + n), s("dd", k0, k1), A.mult)
-        tt(s("cand", k0, k1), s(ps, 256, 256 + n), s("hf", k0, k1), A.add)
-        cp(s("cl", k0, k1), s("cand", k0, k1))
+    def choose(*parts):
+        cut = [("ps%d" % (1 + i), B_CUT[i], B_CUT[i + 1], 128 if B_CUT[i] >= b2 else 0) for i in parts]
+        for ps, k0, k1, p0 in cut:
+            if p0:
+                tt(s(ps, p0, p0 + k1 - k0), s(ps, 0, k1 - k0), s("nh", k0, k1), A.is_equal)
+        for ps, k0, k1, p0 in cut[::-1]:
+            tt(s(ps, 256, 256 + k1 - k0), s(ps, p0, p0 + k1 - k0), s("dd", k0, k1), A.mult)
+        for ps, k0, k1, p0 in cut[::-1]:
+            tt(s("cand", k0, k1), s(ps, 256, 256 + k1 - k0), s("hf", k0, k1), A.add)
+        for ps, k0, k1, p0 in cut[::-1]:
+            cp(s("cl", k0, k1), s("cand", k0, k1))
 
     def name(e, k0, k1):
         take(e, row("wc", k0, k1), at(win("we"), s("cl", k0, k1)))
@@ -348,23 +357,29 @@ def rank_program(g, core, T, topo):
     ask(3)
     tt(s("ps5", 0, K), s("ps0", 0, K), s("eb"), A.not_equal)
     tt(s("dd"), s("ps5", 0, K), s("om"), A.mult)
-    choose(0)
+    acp(s("xc", 0, SL), at(s("xw", 0, V), s("blu")))
+    for d in range(2):
+        shown(s("wbm", 256 * d, 256 * d + 256), s("wb", 256 * d, 256 * d + 256))
+    choose(2, 0)
     name("a", 0, KS)
     a_x3 = exchange("x3", "wc", "wc", GH)
+    exchange("xx", "xc", "xw", V)
     name("a", KS, b1)
     ask(1)
-    choose(2)
     name("a", b2, b3)
-    choose(3)
-    choose(1)
+    cp(s("nbu"), s("nbi"))
+    choose(3, 1)
     name("v", b1, b2)
-    name("a", b3, b3 + B_END // 2)
-    name("v", b3 + B_END // 2, b4)
+    name("a", b3, B_END)
+    name("v", B_END, b4)
     keep("a", "wc", "wc", GH)
-    dmas("y", "lwr", [(s("wr0", rows=slice(c, 128, 16)), hbm(T.w[:, 0:V])) for c in range(16)], [a_x3])
+    keep("a", "xc", "xw", V)
+    dmas("y", "lwr", [(s("wr0", SL, rows=slice(c, 128, 16)), hbm(T.w[:, 0:V])) for c in range(16)], [a_x3])
     dmas("y", "lw8", [(s("w8"), hbm(T.w[:, V:2 * V]))])
     order(KS, b1)
     order(b2, b3)
+    order(b1, b2)
+    order(b3, b4)
     iota(s("yb", DUMP, DUMP + V // 2), [[0, V // 2]], 0, 0)
 
     c0, c1, c2, c3, c4 = C_CUT
@@ -378,36 +393,41 @@ def rank_program(g, core, T, topo):
             acp(row("gat", k0, k1), src)
         to_list(s("ps%d" % (1 + i), 0, k1 - k0), "gat", k0, k1)
 
-    def mates(i):
-        k0, k1 = C_CUT[i:i + 2]
-        ps, n, p0 = "ps%d" % (1 + i), k1 - k0, 0
-        if i > 0:
-            p0 = 128
-            tt(s(ps, p0, p0 + n), s(ps, 0, n), s("eb", k0, k1), A.is_equal)
-        tt(s("mz", k0, k1), s(ps, p0, p0 + n), s("cz", k0, k1), A.mult)
-        ts(s("mo", k0, k1), s("mz", k0, k1), float(ZC), A.add)
+    def mates(*parts, between=()):
+        cut = [("ps%d" % (1 + i), C_CUT[i], C_CUT[i + 1], 128 if i else 0) for i in parts]
+        between = list(between) + [None, None]
+        for ps, k0, k1, p0 in cut:
+            if p0:
+                tt(s(ps, p0, p0 + k1 - k0), s(ps, 0, k1 - k0), s("eb", k0, k1), A.is_equal)
+        if between[0]:
+            between[0]()
+        for ps, k0, k1, p0 in cut:
+            tt(s("mz", k0, k1), s(ps, p0, p0 + k1 - k0), s("cz", k0, k1), A.mult)
+        if between[1]:
+            between[1]()
+        for ps, k0, k1, p0 in cut:
+            op("v", g.vector.tensor_scalar, s("mo", k0, k1), s("mz", k0, k1), -8192.0, float(ZC), A.mult, A.add)
 
     def joined(k0, k1):
         tt(row("fx", k0, k1), at(s("xw"), s("mo", k0, k1)), row("xc", k0, k1), A.add)
 
     answer(0)
     answer(1)
-    ts(s("cz"), s("cand"), -float(ZC), A.add)
+    op("v", g.vector.tensor_scalar, s("cz"), s("cand"), -1.0 / 8192, ZC / 8192, A.mult, A.add)
     fill(s("xw", ZC), 0.0)
-    fill(s("sw", ZC), 0.0)
-    fill(s("wn", ZC), 65536.0)
     fill(s("zz"), 0.0)
-    mates(0)
+    ts(s("icc"), s("igh"), 15, A.bitwise_and)
+    mates(0, between=[None, lambda: fill(s("sw", ZC), 0.0)])
+    fill(s("wn", ZC), 65536.0)
     joined(0, KS)
     exchange("x4", "fx", "fx", GH)
     answer(2)
     answer(3)
-    order(b1, b2)
-    order(b3, b4)
-    joined(KS, c1)
-    mates(1)
-    joined(c1, X_CUT[0])
-    mates(2)
+    mates(1, between=[lambda: joined(KS, 40), lambda: joined(40, c1)])
+    mates(2, between=[lambda: tt(s("ps5", 0, 256), s("ps7", KS, K), s("eb", KS), A.is_ge),
+                      lambda: tt(s("gcol"), s("icc"), s("igh"), A.subtract)])
+    if c1 < X_CUT[0]:
+        joined(c1, X_CUT[0])
     banks = ["ps0", "ps1", "ps2"]
     parts = list(zip(X_CUT, X_CUT[1:]))
     for j, (k0, k1) in enumerate(parts):
@@ -416,44 +436,42 @@ def rank_program(g, core, T, topo):
         mm(s(banks[j], 0, n), [(s("idn"), row("xc", k0, k1)), (s("idn"), s("gx", CH * j, CH * j + n))])
         if j:
             acp(row("fx", *parts[j - 1]), s(banks[j - 1], 0, 16 * (parts[j - 1][1] - parts[j - 1][0])))
-    mates(3)
-    if X_CUT[-1] < c3:
-        joined(X_CUT[-1], c3)
+    mid = (X_CUT[-1] + c3) // 4 * 2
+    mates(3, between=[lambda: joined(X_CUT[-1], mid), lambda: joined(mid, c3)])
+    tt(s("rep"), s("ps5", 0, 256), s("mz", KS), A.is_ge)
+    mm(s("ps6", 0, 256), [(s("bo"), s("rep"))])
+    mm(s("ps6", 256, 512), [(s("nt"), s("rep"))])
     joined(c3, c4)
     acp(row("fx", *parts[-1]), s(banks[-1], 0, 16 * (parts[-1][1] - parts[-1][0])))
     keep("a", "fx", "fx", GH)
 
-    op("v", g.vector.tensor_tensor, s("ge"), s("ps7", KS, K), s("eb", KS), A.is_ge)
-    cp(s("nbu"), s("nbi"))
-    ts(s("ps5", 0, 256), s("ge"), -65536.0, A.mult)
-    tt(s("gcol"), s("icc"), s("igh"), A.subtract)
-    tt(s("rep"), s("mz", KS), s("ps5", 0, 256), A.is_ge)
-    ts(s("ohf"), s("ioa"), 0, A.is_equal)
-    mm(s("ps6", 0, 256), [(s("bo"), s("rep"))])
-    mm(s("ps6", 256, 512), [(s("nt"), s("rep"))])
-    tt(s("tb0"), at(win("fx"), s("hl", 0, KS)), s("wbs", 0, 256), A.mult)
+    mm(s("ps4"), [(s("bo"), s("wbm"))])
+    acp(s("wr0", 0, SL), s("ps4", 0, SL))
+    acp(s("g1", 0, SL), at(win("fx"), s("nbu", K, K + KS)))
     op("v", g.vector.tensor_tensor_scan, s("inc"), s("ps6", 0, 256), s("zz"), float(V * r), A.add, A.add)
-    tt(s("tb1"), at(win("fx"), s("ob")), s("wbs", 256, 512), A.mult)
+    tt(s("s5"), at(win("fx"), s("nbu", 0, KS)), s("wr0", 0, SL), A.mult)
     tt(s("num"), s("inc"), s("ps6", 256, 512), A.subtract)
-    tt(s("s5"), s("tb0"), s("tb1"), A.add)
-    exchange("x5", "s5", "sw", V)
+    tt(s("ps5", 0, SL), s("g1", 0, SL), s("ps4", SL), A.mult)
     shown(s("s6"), s("num"))
+    tt(s("s5"), s("s5"), s("ps5", 0, SL), A.add)
     exchange("x6", "s6", "wn", V)
+    exchange("x5", "s5", "sw", V)
+    ts(s("ohf"), s("ioa"), 0, A.is_equal)
 
     NC, KC = V // CH, CH // 16
     for i in range(NC + 2):
         if i < NC:
             lo, hi = CH * i, CH * i + CH
-            acp(s("g1", lo, hi), at(win("fx"), s("nbu", 256 + KC * i, 256 + KC * (i + 1))))
+            acp(s("g1", SL + lo, SL + hi), at(win("fx"), s("nbu", K + KS + KC * i, K + KS + KC * (i + 1))))
             mm(s("ps%d" % (i % 2)), [(s("r8"), s("w8", lo, hi))])
-            tt(s("sw", lo, hi), at(win("fx"), s("nbu", KC * i, KC * (i + 1))), s("wr0", lo, hi), A.mult)
+            tt(s("sw", lo, hi), at(win("fx"), s("nbu", KS + KC * i, KS + KC * (i + 1))), s("wr0", SL + lo, SL + hi), A.mult)
         k = i - 1
         if 0 <= k < NC:
             lo, hi = CH * k, CH * k + CH
-            dst = s("g1", lo, hi) if k in DMA_CHUNKS else s("ps%d" % (2 + k % 3))
-            tt(dst, s("g1", lo, hi), s("ps%d" % (k % 2)), A.mult)
+            dst = s("g1", SL + lo, SL + hi) if k in DMA_CHUNKS else s("ps%d" % (2 + k % 3))
+            tt(dst, s("g1", SL + lo, SL + hi), s("ps%d" % (k % 2)), A.mult)
             if k in DMA_CHUNKS:
-                dmas("g", "ad%d" % k, [(s("sw", lo, hi), s("g1", lo, hi))], accum_op=A.add)
+                dmas("g", "ad%d" % k, [(s("sw", lo, hi), s("g1", SL + lo, SL + hi))], accum_op=A.add)
         k = i - 2
         if 0 <= k < NC and k not in DMA_CHUNKS:
             lo, hi = CH * k, CH * k + CH

import numpy as np
from concourse.bass import DstId, RemoteDMATransfer
from concourse.mybir import AluOpType, ActivationFunctionType

V, C, N = 4096, 64, 4
SL = N * C
KS = SL // 16
K = KS + V // 16
GH = V + SL
ZC = GH
CH = 512
DUMP = 512
DMA_CHUNKS = (0, 1, 2)
N_V = 128
A_CUT = (16, 80, 140, 206, K)
B_CUT = (0, 64, 128, 200, K)
B_END = 248
C_CUT = (0, 64, 136, 208, K)
X_CUT = (64, 92, 120, 148)
COARSE = {-1: (0, 1), 2: (2,), 4: (3,)}

SCRATCH = {}


def _declare(names, cols, dtype, rows=128):
    for n in names.split():
        SCRATCH[n] = ("sbuf", [rows, cols] if isinstance(cols, int) else [rows] + list(cols), dtype)


_declare("bli ioh ioa bla blb", 16, "int32")
_declare("blu blh bl15", 16, "uint16")
_declare("blg tl", 32, "uint16")
_declare("ti", 32, "int32")
_declare("z2", (16, 32), "bfloat16")
_declare("nbi", 2 * K, "int32")
_declare("nbu", 2 * K, "uint16")
_declare("z", (2, 16, 16), "bfloat16")
_declare("wb wbm wt", 512, "bfloat16")
_declare("hl cl mo", K, "uint16")
_declare("hf om dd cand cz mz nh", K, "float32")
_declare("eb pf sg", K, "bfloat16")
_declare("pos", 256, "uint16")
_declare("num inc cms idm dm zz s5 s6 ge", 256, "float32")
_declare("nbm", 512, "float32")
_declare("rep blm pfm", 256, "bfloat16")
_declare("ohf", 16, "float32")
_declare("ohb", 16, "bfloat16")
_declare("igh icc", 2, "int32")
_declare("gcol", 2, "float32")
_declare("r8", 128, "bfloat16", 8)
_declare("sel oneb", 144, "bfloat16")
_declare("one", 144, "float32")
_declare("bo nt idn e0", 128, "bfloat16")
_declare("we wa wh wc", SL + GH, "bfloat16")
_declare("gat xc wr0", SL + V, "bfloat16")
_declare("gx", V, "bfloat16")
_declare("fx", SL + GH, "float32")
_declare("wn sw", GH + 16, "float32")
_declare("gatn", V, "float32")
_declare("g1", SL + V, "float32")
_declare("xw", GH + 16, "bfloat16")
_declare("w8", V, "bfloat16", 8)
_declare("yb", DUMP + V, "float32")
for _i in range(8):
    SCRATCH["ps%d" % _i] = ("psum", [128, 512], "float32")

EXCH = ["x0", "x1", "x2", "x3", "xx", "x4", "x5", "x6"]
LOADS = ["lbl", "lnb", "lw", "lx", "lxc", "lwr", "lw8", "lr8", "sty", "stc"] + ["ad%d" % k for k in range(8)]
SEMAPHORES = ["v", "a", "t", "q", "sent"] + EXCH + LOADS


def link_engines(topo, cores, src):
    on = [d for d in cores if d != src and topo.chip(d) == topo.chip(src)]
    off = [d for d in cores if d != src and topo.chip(d) != topo.chip(src)]
    out, used = {}, []
    for d in off + on:
        left = [e for e in topo.engines(src, d) if e not in used]
        if d in on and off:
            far = topo.engines(src, off[0])
            left = [e for e in left if e not in far] or left
        out[d] = left[:4]
        used += out[d]
    return out


def rank_program(g, core, T, topo):
    r = T.rank_of(core)
    if r is None:
        return
    A = AluOpType
    COPY = ActivationFunctionType.Copy
    IDENT = ActivationFunctionType.Identity
    cores = list(T.cores)
    Q = {"v": g.vector, "a": g.scalar, "t": g.tensor, "g": g, "y": g.sync}
    SEM = {"v": "v", "a": "a", "t": "t", "g": "q"}
    cnt = {s: 0 for s in SEMAPHORES}
    seen = {}
    touched = {n: [] for n in SCRATCH}

    def s(name, lo=0, hi=None, step=1, rows=None):
        hi = SCRATCH[name][1][1] if hi is None else hi
        return (T[name][slice(None) if rows is None else rows, lo:hi:step], [(name, lo, hi)])

    def at(win, lst):
        return (win[0].indirect(lst[0]), win[1], lst[1])

    def hbm(ap):
        return (ap, [])

    def wait(qn, deps):
        best = {}
        for sem, n in deps:
            best[sem] = max(best.get(sem, 0), cnt[sem] if sem in LOADS else n)
        for sem, n in best.items():
            if seen.get((qn, sem), 0) < n:
                Q[qn].wait_ge(T.sem[sem], n)
                seen[(qn, sem)] = n

    def spans(outs, ins):
        views = [x for x in ins if isinstance(x, tuple)]
        return [x for o in outs for x in o[1]], [x for i in views for x in i[1]] + [x for i in outs + views if len(i) > 2 for x in i[2]]

    def hazards(qn, outs, ins):
        wr, rd = spans(outs, ins)
        deps = []
        for group, writing in ((wr, True), (rd, False)):
            for name, lo, hi in group:
                bank = SCRATCH[name][0] == "psum"
                deps += [tok for a, b, tok, q, w in touched[name]
                         if (bank and q != qn) or (a < hi and lo < b and (w or writing))]
        return deps

    def record(qn, outs, ins, tok):
        wr, rd = spans(outs, ins)
        for name, lo, hi in rd:
            touched[name].append((lo, hi, tok, qn, False))
        for name, lo, hi in wr:
            touched[name].append((lo, hi, tok, qn, True))
        return tok

    def ap(x):
        return x[0] if isinstance(x, tuple) else x

    def side_by_side(qn, calls):
        wait(qn, [d for fn, out, args, kw in calls for d in hazards(qn, [out], list(args) + list(kw.values()))])
        for fn, out, args, kw in calls:
            fn(ap(out), *[ap(x) for x in args], **{k: ap(x) for k, x in kw.items()}).then_inc(T.sem[SEM[qn]], 1)
            cnt[SEM[qn]] += 1
        for fn, out, args, kw in calls:
            record(qn, [out], list(args) + list(kw.values()), (SEM[qn], cnt[SEM[qn]]))

    def op(qn, fn, out, *args, **kw):
        side_by_side(qn, [(fn, out, args, kw)])

    def dmas(qn, sem, pairs, after=(), **kw):
        wait(qn, [d for o, i in pairs for d in hazards(qn, [o], [i])] + list(after))
        for o, i in pairs:
            Q[qn].dma_start(ap(o), ap(i), **kw).then_inc(T.sem[sem], 16)
            cnt[sem] += 16
        for o, i in pairs:
            record(sem, [o], [i], (sem, cnt[sem]))

    def mm(out, terms):
        ins = [x for t in terms for x in t]
        wait("t", hazards("t", [out], ins))
        for i, (l, x) in enumerate(terms):
            call = g.tensor.matmul(ap(out), ap(l), ap(x), i == 0, i == len(terms) - 1)
        call.then_inc(T.sem.t, 1)
        cnt["t"] += 1
        record("t", [out], ins, ("t", cnt["t"]))

    def tt(o, a, b, f):
        op("v", g.vector.tensor_tensor, o, a, b, f)

    def ts(o, a, s1, f):
        op("v", g.vector.tensor_scalar, o, a, s1, None, f)

    def cp(o, a):
        op("v", g.vector.tensor_copy, o, a)

    def fill(o, c):
        op("v", g.vector.memset, o, c)

    def acp(o, a, **kw):
        op("a", g.scalar.activation, o, a, COPY, **kw)

    def plus(o, a, b, **kw):
        op("a", g.scalar.activation, o, a, IDENT, bias=b, **kw)

    def take(e, o, a):
        cp(o, a) if e == "v" else acp(o, a)

    def iota(o, pattern, base, step):
        op("g", g.iota, o, pattern, base, step, allow_small_or_imprecise_dtypes=True)

    def select(o, a, pattern, f, base, step):
        op("g", g.affine_select, o, a, pattern, f, 0.0, base, step)

    mine = link_engines(topo, cores, core)

    def exchange(sem, src, dst, d0, width=C, pitch=C):
        pieces = [s(src, width * q, width * q + width) for q in range(N)]
        wait("g", hazards("g", [], pieces))
        tr = []
        for q in range(N):
            if q != r:
                a = topo.addr(cores[q])
                tr.append(RemoteDMATransfer(dst_ids=[DstId(rid=a[0], pnc=a[1])], remote_sem=T.sem[sem],
                                            dma_engine_mask=sum(1 << e for e in mine[cores[q]]), srcs=[ap(pieces[q])],
                                            dsts=[ap(s(dst, d0 + pitch * r, d0 + pitch * r + width))]))
        g.remote_dma_fused(tr, local_sem=T.sem.sent)
        cnt["sent"] += sum(len(mine[d]) for d in mine)
        cnt[sem] += sum(len(link_engines(topo, cores, c)[core]) for c in cores if c != core)
        record(sem, [s(dst, d0 + pitch * q, d0 + pitch * q + width) for q in range(N) if q != r], [], (sem, cnt[sem]))
        return (sem, cnt[sem])

    def keep(e, src, dst, d0):
        take(e, s(dst, d0 + C * r, d0 + C * r + C), s(src, C * r, C * r + C))

    def win(name):
        return s(name, SL, SL + GH)

    def row(name, k0, k1):
        return s(name, 16 * k0, 16 * k1)

    def to_list(out, src, k0, k1, sel="sel"):
        mm(out, [(s(sel, 15 - c, 143 - c), s(src, 16 * k0 + c, 16 * k1, 16)) for c in range(16)])

    def shown(out, tile):
        tt(out, at(tile, s("blh")), s("blm"), A.mult)

    dmas("y", "lbl", [(s("bli"), hbm(T.bl[:]))])
    dmas("y", "lnb", [(s("nbi", K * d + KS, K * d + K), hbm(T.nb[:, 256 * d:256 * d + 256])) for d in range(2)])
    dmas("a", "lw", [((T.z[:, h], [("z", h, h + 1)]), hbm(T.w[h::2, :])) for h in range(2)])

    iota(s("e0"), [[1, 128]], 128, 0)
    op("g", g.iota, s("ioh"), [[-1, 16]], 16, 1)
    op("g", g.iota, s("ti"), [[1, 32]], 0, 32)
    fill(s("one"), 0.0)
    fill(s("one", 15, 143, 16), 1.0)
    select(s("one", 15, 143, 16), s("one", 15, 143, 16), [[-16, 8]], A.is_ge, 0, 1)
    select(s("one", 15, 143, 16), s("one", 15, 143, 16), [[16, 8]], A.is_ge, 15, -1)
    E0 = 32 * r - 71
    ts(s("we", SL, SL + 128), s("e0"), 2.0 ** E0, A.mult)
    ts(s("we", SL + 128, SL + 256), s("e0"), 2.0 ** (E0 + 1), A.mult)
    ts(s("we", SL + 256, SL + 512), s("we", SL, SL + 256), 4.0, A.mult)
    ts(s("ioa"), s("ioh"), 15, A.bitwise_and)
    ts(s("we", SL + 512, SL + 1024), s("we", SL, SL + 512), 16.0, A.mult)
    ts(s("ti"), s("ti"), 511, A.bitwise_and)
    ts(s("ohb"), s("ioa"), 0, A.is_equal)
    cp(s("tl"), s("ti"))
    cp(s("blu"), s("bli"))
    a_x0 = exchange("x0", "blu", "blg", 0, width=4, pitch=8)
    op("g", g.iota, s("igh"), [[0, 2]], 0, 1)
    iota(s("bo"), [[0, 128]], 1, 0)
    select(s("bo"), s("bo"), [[-16, 8], [0, 16]], A.is_ge, 0, 1)
    select(s("bo"), s("bo"), [[16, 8], [0, 16]], A.is_ge, 15, -1)
    iota(s("idm"), [[0, 8], [16, 32]], 0, 1)
    select(s("nt"), s("bo"), [[-1, 128]], A.is_ge, 0, 1)
    select(s("idn"), s("bo"), [[-1, 128]], A.is_equal, 0, 1)

    def names(n):
        acp(s("we", SL + n, SL + n + 1024), s("we", SL, SL + 1024), scale=2.0 ** (n // 128))

    names(1024)
    side_by_side("a", [(g.scalar.activation, (T.z2[:, :, 16 * h:16 * h + 16], [("z2", 0, 1)]), [(T.z[:, h], [("z", h, h + 1)]), COPY], {})
                       for h in range(2)])
    acp(s("oneb"), s("one"))
    ts(s("blb"), s("bli"), 15, A.bitwise_and)
    ts(s("bla"), s("bli"), 4, A.arith_shift_right)
    cp(s("bl15"), s("blb"))
    cp(s("blh"), s("bla"))
    cp(s("blm"), at(s("ohb"), s("bl15")))
    op("v", g.vector.transpose, s("wt"), (T.z2[:], [("z2", 0, 1)]))
    acp(s("wb", 256), at(s("wt"), s("tl", 16)))
    cp(s("wb", 0, 256), at(s("wt"), s("tl", 0, 16)))
    names(2048)
    names(3072)
    acp(s("we", 0, SL), at(s("we", SL, GH), s("blu")))
    acp(s("sel"), s("one"), scale=0.0625)
    keep("a", "we", "we", GH)
    for d in range(2):
        shown(s("nbm", 256 * d, 256 * d + 256), s("nbi", K * d + KS, K * d + K))
    to_list(s("ps6", 0, 2 * KS), "nbm", 0, 2 * KS, "one")
    tt(s("pf", KS), s("wb", 0, 256), s("wb", 256, 512), A.is_ge)
    tt(s("ps5", KS, K), s("nbi", KS, K), s("nbi", K + KS), A.subtract)
    shown(s("pfm"), s("pf", KS))
    to_list(s("ps3", 0, KS), "pfm", 0, KS, "oneb")
    to_list(s("ps7", 0, K), "we", 0, K)
    tt(s("ps4", KS, K), s("pf", KS), s("ps5", KS, K), A.mult)
    tt(s("hf", KS), s("nbi", K + KS), s("ps4", KS, K), A.add)
    cp(s("hl", KS), s("hf", KS))
    for d in range(2):
        cp(s("nbi", K * d, K * d + KS), s("ps6", KS * d, KS * d + KS))
    cp(s("pf", 0, KS), s("ps3", 0, KS))
    tt(s("ps5", 0, KS), s("nbi", 0, KS), s("nbi", K, K + KS), A.subtract)
    tt(s("ps4", 0, KS), s("pf", 0, KS), s("ps5", 0, KS), A.mult)
    tt(s("hf", 0, KS), s("nbi", K, K + KS), s("ps4", 0, KS), A.add)
    cp(s("hl", 0, KS), s("hf", 0, KS))
    for q in range(N):
        if q != r:
            acp(s("we", GH + C * q, GH + C * q + C), at(s("we", SL, GH), s("blg", 8 * q, 8 * q + 4)), scale=2.0 ** (32 * (q - r)))
    dmas("y", "lx", [(s("xw", 0, V), hbm(T.x[:]))], [a_x0])
    dmas("y", "lr8", [(s("r8"), s("bo", rows=slice(0, 128, 16)))])

    b0, b1, b2, b3, b4 = B_CUT
    acp(row("wa", N_V, K), at(win("we"), s("hl", N_V)))
    cp(row("wa", 0, KS), at(win("we"), s("hl", 0, KS)))
    a_x1 = exchange("x1", "wa", "wa", GH)
    cp(row("wa", KS, N_V), at(win("we"), s("hl", KS, N_V)))
    to_list(s("ps2", 0, K - b2), "wa", b2, K)
    keep("v", "wa", "wa", GH)
    plus(s("sg"), s("pf"), 1.0, scale=-2.0)
    acp(s("eb"), s("ps7", 0, K))

    cp(row("wh", 0, KS), at(win("wa"), s("hl", 0, KS)))
    a_x2 = exchange("x2", "wh", "wh", GH)
    dmas("y", "lxc", [(s("xc", SL), hbm(T.x[:]))], [a_x2])
    a0, a1, a2, a3, a4 = A_CUT
    for e, k0, k1, p0 in (("a", a2, a3, a2), ("v", a0, a1, 0), ("a", a3, a4, a3), ("v", a1, a2, a1)):
        take(e, row("wh", k0, k1), at(win("wa"), s("hl", k0, k1)))
        to_list(s("ps0", p0, k1), "wh", p0, k1)
        if k0 == a0:
            tt(s("om"), s("sg"), s("ps5", 0, K), A.mult)
    keep("v", "wh", "wh", GH)
    acp(s("nh", b2), s("ps2", 0, K - b2))

    def ask(i):
        k0, k1 = B_CUT[i:i + 2]
        src = at(win("wh"), s("hl", k0, k1))
        if k0 >= b2:
            acp(row("gat", k0, k1), src)
        else:
            tt(row("gat", k0, k1), src, row("wa", k0, k1), A.is_equal)
        to_list(s("ps%d" % (1 + i), 0, k1 - k0), "gat", k0, k1)

    def choose(*parts):
        cut = [("ps%d" % (1 + i), B_CUT[i], B_CUT[i + 1], 128 if B_CUT[i] >= b2 else 0) for i in parts]
        for ps, k0, k1, p0 in cut:
            if p0:
                tt(s(ps, p0, p0 + k1 - k0), s(ps, 0, k1 - k0), s("nh", k0, k1), A.is_equal)
        for ps, k0, k1, p0 in cut[::-1]:
            tt(s(ps, 256, 256 + k1 - k0), s(ps, p0, p0 + k1 - k0), s("dd", k0, k1), A.mult)
        for ps, k0, k1, p0 in cut[::-1]:
            tt(s("cand", k0, k1), s(ps, 256, 256 + k1 - k0), s("hf", k0, k1), A.add)
        for ps, k0, k1, p0 in cut[::-1]:
            cp(s("cl", k0, k1), s("cand", k0, k1))

    def name(e, k0, k1):
        take(e, row("wc", k0, k1), at(win("we"), s("cl", k0, k1)))

    def order(k0, k1):
        to_list(s("ps7", k0, k1), "wc", k0, k1)

    ask(0)
    ask(2)
    ask(3)
    tt(s("ps5", 0, K), s("ps0", 0, K), s("eb"), A.not_equal)
    tt(s("dd"), s("ps5", 0, K), s("om"), A.mult)
    acp(s("xc", 0, SL), at(s("xw", 0, V), s("blu")))
    for d in range(2):
        shown(s("wbm", 256 * d, 256 * d + 256), s("wb", 256 * d, 256 * d + 256))
    choose(2, 0)
    name("a", 0, KS)
    a_x3 = exchange("x3", "wc", "wc", GH)
    exchange("xx", "xc", "xw", V)
    name("a", KS, b1)
    ask(1)
    name("a", b2, b3)
    cp(s("nbu"), s("nbi"))
    choose(3, 1)
    name("v", b1, b2)
    name("a", b3, B_END)
    name("v", B_END, b4)
    keep("a", "wc", "wc", GH)
    keep("a", "xc", "xw", V)
    dmas("y", "lwr", [(s("wr0", SL, rows=slice(c, 128, 16)), hbm(T.w[:, 0:V])) for c in range(16)], [a_x3])
    dmas("y", "lw8", [(s("w8"), hbm(T.w[:, V:2 * V]))])
    order(KS, b1)
    order(b2, b3)
    order(b1, b2)
    order(b3, b4)
    iota(s("yb", DUMP, DUMP + V // 2), [[0, V // 2]], 0, 0)

    c0, c1, c2, c3, c4 = C_CUT

    def answer(i):
        k0, k1 = C_CUT[i:i + 2]
        src = at(win("wc"), s("cl", k0, k1))
        if i == 0:
            tt(row("gat", k0, k1), src, row("we", k0, k1), A.is_equal)
        else:
            acp(row("gat", k0, k1), src)
        to_list(s("ps%d" % (1 + i), 0, k1 - k0), "gat", k0, k1)

    def mates(*parts, between=()):
        cut = [("ps%d" % (1 + i), C_CUT[i], C_CUT[i + 1], 128 if i else 0) for i in parts]
        between = list(between) + [None, None]
        for ps, k0, k1, p0 in cut:
            if p0:
                tt(s(ps, p0, p0 + k1 - k0), s(ps, 0, k1 - k0), s("eb", k0, k1), A.is_equal)
        if between[0]:
            between[0]()
        for ps, k0, k1, p0 in cut:
            tt(s("mz", k0, k1), s(ps, p0, p0 + k1 - k0), s("cz", k0, k1), A.mult)
        if between[1]:
            between[1]()
        for ps, k0, k1, p0 in cut:
            op("v", g.vector.tensor_scalar, s("mo", k0, k1), s("mz", k0, k1), -8192.0, float(ZC), A.mult, A.add)

    def joined(k0, k1):
        tt(row("fx", k0, k1), at(s("xw"), s("mo", k0, k1)), row("xc", k0, k1), A.add)

    answer(0)
    answer(1)
    op("v", g.vector.tensor_scalar, s("cz"), s("cand"), -1.0 / 8192, ZC / 8192, A.mult, A.add)
    fill(s("xw", ZC), 0.0)
    fill(s("zz"), 0.0)
    ts(s("icc"), s("igh"), 15, A.bitwise_and)
    mates(0, between=[None, lambda: fill(s("sw", ZC), 0.0)])
    fill(s("wn", ZC), 65536.0)
    joined(0, KS)
    exchange("x4", "fx", "fx", GH)
    answer(2)
    answer(3)
    mates(1, between=[lambda: joined(KS, 40), lambda: joined(40, c1)])
    mates(2, between=[lambda: tt(s("ps5", 0, 256), s("ps7", KS, K), s("eb", KS), A.is_ge),
                      lambda: tt(s("gcol"), s("icc"), s("igh"), A.subtract)])
    if c1 < X_CUT[0]:
        joined(c1, X_CUT[0])
    banks = ["ps0", "ps1", "ps2"]
    parts = list(zip(X_CUT, X_CUT[1:]))
    for j, (k0, k1) in enumerate(parts):
        n = 16 * (k1 - k0)
        acp(s("gx", CH * j, CH * j + n), at(s("xw"), s("mo", k0, k1)))
        mm(s(banks[j], 0, n), [(s("idn"), row("xc", k0, k1)), (s("idn"), s("gx", CH * j, CH * j + n))])
        if j:
            acp(row("fx", *parts[j - 1]), s(banks[j - 1], 0, 16 * (parts[j - 1][1] - parts[j - 1][0])))
    mid = (X_CUT[-1] + c3) // 4 * 2
    mates(3, between=[lambda: joined(X_CUT[-1], mid), lambda: joined(mid, c3)])
    tt(s("rep"), s("ps5", 0, 256), s("mz", KS), A.is_ge)
    mm(s("ps6", 0, 256), [(s("bo"), s("rep"))])
    mm(s("ps6", 256, 512), [(s("nt"), s("rep"))])
    joined(c3, c4)
    acp(row("fx", *parts[-1]), s(banks[-1], 0, 16 * (parts[-1][1] - parts[-1][0])))
    keep("a", "fx", "fx", GH)

    mm(s("ps4"), [(s("bo"), s("wbm"))])
    acp(s("wr0", 0, SL), s("ps4", 0, SL))
    acp(s("g1", 0, SL), at(win("fx"), s("nbu", K, K + KS)))
    op("v", g.vector.tensor_tensor_scan, s("inc"), s("ps6", 0, 256), s("zz"), float(V * r), A.add, A.add)
    tt(s("s5"), at(win("fx"), s("nbu", 0, KS)), s("wr0", 0, SL), A.mult)
    tt(s("num"), s("inc"), s("ps6", 256, 512), A.subtract)
    tt(s("ps5", 0, SL), s("g1", 0, SL), s("ps4", SL), A.mult)
    shown(s("s6"), s("num"))
    tt(s("s5"), s("s5"), s("ps5", 0, SL), A.add)
    exchange("x6", "s6", "wn", V)
    exchange("x5", "s5", "sw", V)
    ts(s("ohf"), s("ioa"), 0, A.is_equal)

    NC, KC = V // CH, CH // 16
    for i in range(NC + 2):
        if i < NC:
            lo, hi = CH * i, CH * i + CH
            acp(s("g1", SL + lo, SL + hi), at(win("fx"), s("nbu", K + KS + KC * i, K + KS + KC * (i + 1))))
            mm(s("ps%d" % (i % 2)), [(s("r8"), s("w8", lo, hi))])
            tt(s("sw", lo, hi), at(win("fx"), s("nbu", KS + KC * i, KS + KC * (i + 1))), s("wr0", SL + lo, SL + hi), A.mult)
        k = i - 1
        if 0 <= k < NC:
            lo, hi = CH * k, CH * k + CH
            dst = s("g1", SL + lo, SL + hi) if k in DMA_CHUNKS else s("ps%d" % (2 + k % 3))
            tt(dst, s("g1", SL + lo, SL + hi), s("ps%d" % (k % 2)), A.mult)
            if k in DMA_CHUNKS:
                dmas("g", "ad%d" % k, [(s("sw", lo, hi), s("g1", SL + lo, SL + hi))], accum_op=A.add)
        k = i - 2
        if 0 <= k < NC and k not in DMA_CHUNKS:
            lo, hi = CH * k, CH * k + CH
            tt(s("sw", lo, hi), s("sw", lo, hi), s("ps%d" % (2 + k % 3)), A.add)
    iota(s("yb", DUMP + V // 2), [[0, V // 2]], 0, 0)
    keep("a", "s5", "sw", V)
    keep("a", "s6", "wn", V)
    plus(s("dm"), s("idm"), s("gcol", 0, 1))
    plus(s("ps6", 0, 256), s("num"), float(DUMP - V * r))
    side_by_side("a", [(g.scalar.activation, s("wn", c, V, 16), [s("num"), COPY], {"scale": s("ohf", c, c + 1)}) for c in range(16)])

    def coarse(n):
        for j in COARSE.get(n, ()):
            acp(s("gatn", 1024 * j, 1024 * j + 1024), at(s("wn"), s("mo", KS + 64 * j, KS + 64 * j + 64)))
            to_list(s("ps7", 64 * j, 64 * j + 64), "gatn", 64 * j, 64 * j + 64, "one")

    coarse(-1)
    tt(s("inc"), s("rep"), s("ps6", 0, 256), A.mult)
    tt(s("ps5", 0, 256), s("inc"), s("dm"), A.max)
    cp(s("pos"), s("ps5", 0, 256))

    cuts = [CH * i for i in range(NC, 0, -1)] + [128, 0]
    for n, (hi, lo) in enumerate(zip(cuts, cuts[1:])):
        acp(s("g1", lo, hi), at(s("sw"), s("mo", KS + lo // 16, KS + hi // 16)))
        tt(at(s("yb", 0, DUMP + hi), s("pos", lo // 16, hi // 16)), s("sw", lo, hi), s("g1", lo, hi), A.add)
        dmas("y", "sty", [(hbm(T.y[:, lo:hi]), s("yb", DUMP + lo, DUMP + hi))])
        coarse(n)
        if n == 7:
            tt(s("cms"), s("ps7", 0, 256), s("num"), A.min)
            dmas("y", "stc", [(hbm(T.cm[:]), s("cms"))])
    wait("y", [(n, cnt[n]) for n in SEMAPHORES if cnt[n]])
